import numpy as np
import ml_dtypes


def mxq(x, axis, fmt="e4m3"):
    dtype, down = {"e4m3": (ml_dtypes.float8_e4m3fn, 7), "e5m2": (ml_dtypes.float8_e5m2, 14)}[fmt]
    v = np.moveaxis(np.asarray(x, np.float32).astype(ml_dtypes.bfloat16).astype(np.float64), axis, -1)
    blocks = v.reshape(v.shape[:-1] + (-1, 32))
    amax = np.abs(blocks).max(-1, keepdims=True)
    byte = np.maximum(np.where(amax > 0, np.frexp(amax)[1] - 1 + 127, 0) - down, 1)
    scale = np.exp2(byte - 127.0)
    codes = (blocks / scale).astype(np.float32).astype(dtype).astype(np.float64)
    return np.moveaxis((codes * scale).reshape(v.shape), -1, axis)


WIDE = False


def mx_kscale(k):
    if not WIDE:
        return np.ones(k)
    levels = np.array([10, -10, 5, -5, 0])
    if k % 512:
        return np.exp2(np.random.permutation(np.resize(levels, k // 32))).repeat(32)
    a = np.empty((k // 512, 16))
    for p in range(k // 512):
        a[p, :8] = np.random.permutation(np.resize(levels, 8))
        for g in range(8):
            far = levels[np.abs(levels - a[p, g]) >= 10]
            a[p, g + 8] = far[np.random.randint(len(far))]
    return np.exp2(a.ravel()).repeat(32)


def f64(x):
    return np.asarray(x).astype(np.float64)


def striped(idx):
    return np.tile(idx.reshape(-1, 16).T, (8, 1)).astype(np.uint16)


def unstriped(offs):
    return offs[:16].T.reshape(-1).astype(np.int64)


def pack_weight(w):
    k, n = w.shape
    w = f64(np.asarray(w, np.float32).astype(ml_dtypes.bfloat16)).reshape(k // 32, 32, n)
    amax = np.abs(w).max(1)
    byte = np.clip(np.where(amax > 0, np.frexp(amax)[1] - 1 + 127 - 7, 1), 1, 254)
    scaled = (w * np.exp2(127.0 - byte)[:, None, :]).reshape(k, n).astype(np.float32)
    words = np.ascontiguousarray(scaled.reshape(k // 512, 128, 4, n).transpose(0, 1, 3, 2)).astype(ml_dtypes.float8_e4m3fn).view(np.uint8)
    return words, np.ascontiguousarray(byte.astype(np.uint8).reshape(k // 512, 16, n))


def unpack_weight(words, scales):
    g, p, n, _ = words.shape
    vals = np.ascontiguousarray(words).view(ml_dtypes.float8_e4m3fn).astype(np.float64) * np.repeat(np.exp2(scales.astype(np.float64) - 127.0), 8, axis=1)[..., None]
    return vals.transpose(0, 1, 3, 2).reshape(g * 512, n)


def sigmoid(v):
    return 1.0 / (1.0 + np.exp(-np.maximum(v, -700.0)))


K, T, S, N = 1024, 2048, 1024, 256


def setup_inputs():
    n = np.random.standard_normal
    s = mx_kscale(K)[:, None]
    packed_w1 = pack_weight(n((K, N)) / np.sqrt(K) / s)
    packed_w2 = pack_weight(n((K, N)) / np.sqrt(K) / s)
    return {
        "xT": (n((K, T)) * s).astype(np.float32),
        "res": n((N, T)).astype(np.float32),
        "w1_words": packed_w1[0],
        "w1_scales": packed_w1[1],
        "w2_words": packed_w2[0],
        "w2_scales": packed_w2[1],
        "offs": striped(np.random.permutation(T)[:S]),
    }


def reference(xT, res, w1_words, w1_scales, w2_words, w2_scales, offs):
    r = f64(res)[:, unstriped(offs)]
    xq = mxq(f64(xT)[:, unstriped(offs)], 0, "e4m3")
    g = sigmoid(unpack_weight(w2_words, w2_scales).T @ xq)
    y = np.tanh(unpack_weight(w1_words, w1_scales).T @ xq)
    return r + g * (y - r)

@@ -1,0 +1,173 @@
+from contextlib import ExitStack
+
+import concourse.mybir as mybir
+
+K, T, S, N = 1024, 2048, 1024, 256
+FLOPS = 2 * 2 * K * N * S
+
+F32 = mybir.dt.float32
+BF16 = mybir.dt.bfloat16
+I32 = mybir.dt.int32
+U32 = mybir.dt.uint32
+U16 = mybir.dt.uint16
+U8 = mybir.dt.uint8
+FP8X4 = mybir.dt.float8_e4m3fn_x4
+ALU = mybir.AluOpType
+TANH = mybir.ActivationFunctionType.Tanh
+
+P = 128
+HALF = 512
+PIECE = 256
+CHUNKS = [[(1024, 0), (1024, 672)], [(1024, 0), (1024, 672)], [(1024, 0), (512, 0), (512, 320)], [(1024, 0), (512, 512), (512, 320)]]
+
+
+def tile_picked_highway_tanh_l_kernel(
+    tc, xT, res, w1_words, w1_scales, w2_words, w2_scales, offs, out
+):
+    nc = tc.nc
+    with ExitStack() as ctx:
+        keep = ctx.enter_context(tc.tile_pool(name="keep", bufs=1))
+        work = ctx.enter_context(tc.tile_pool(name="work", bufs=4))
+        psum = ctx.enter_context(tc.psum_pool(name="psum", bufs=8))
+
+        offsets = keep.tile([P, S // 16], U16, name="offsets")
+
+        def entries(j0, n):
+            return offsets[:, j0 // 16 : (j0 + n) // 16]
+
+        zero_in = keep.tile([P, 1], F32, name="zero_in")
+        zero = keep.tile([P, 1], F32, name="zero")
+        nc.vector.memset(zero_in[:], 0.0)
+        nc.scalar.activation(zero[:], zero_in[:], TANH)
+
+        w_scale = keep.tile([P, N], U8, name="w_scale", align_bytes=64)
+        nc.gpsimd.memset(w_scale[:].bitcast(I32), 0)
+        for w, scales in enumerate((w1_scales, w2_scales)):
+            for q in range(4):
+                nc.gpsimd.dma_start(
+                    out=w_scale[32 * q + 8 * w : 32 * q + 8 * w + 8, :].bitcast(I32),
+                    in_=scales.bitcast(I32)[:, 4 * q : 4 * q + 4, :],
+                )
+
+        x_rows = xT.rearrange("(z p t) c -> z p t c", p=P, t=4)
+        raw = {}
+        for pair in range(4):
+            z, h = divmod(pair, 2)
+            c0 = 0
+            for i, (width, v_cols) in enumerate(CHUNKS[pair]):
+                raw[pair, i] = keep.tile([P, 2, width], F32, name="raw%d_%d" % (pair, i))
+                nc.sync.dma_start(out=raw[pair, i][:], in_=x_rows[z, :, 2 * h : 2 * h + 2, c0 : c0 + width])
+                if pair == 0 and i == 0:
+                    nc.sync.dma_start(offsets[:], offs)
+                c0 += width
+        w_codes = []
+        for w, words in enumerate((w1_words, w2_words)):
+            codes = keep.tile([P, 2, N], I32, name="w_codes%d" % w, align_bytes=64)
+            nc.sync.dma_start(out=codes[:], in_=words.rearrange("z p n t -> p z (n t)").bitcast(I32))
+            w_codes.append(codes)
+        res_rows = []
+        for b in range(2):
+            rows = keep.tile([P, T], F32, name="res%d" % b)
+            nc.sync.dma_start(out=rows[:], in_=res[P * b : P * (b + 1), :])
+            res_rows.append(rows)
+
+        picked = {}
+        x_codes = {}
+        x_scale = {}
+        for z in range(2):
+            for half in range(2):
+                picked[z, half] = keep.tile([P, 2, HALF], U32, name="picked%d_%d" % (z, half))
+                x_codes[z, half] = keep.tile([P, HALF], U32, name="x_codes%d_%d" % (z, half), align_bytes=64)
+                x_scale[z, half] = keep.tile([P, HALF], U8, name="x_scale%d_%d" % (z, half), align_bytes=64)
+
+        def cast(pair):
+            window = keep.tile([P, 2 * T], BF16, name="window%d" % pair)
+            c0 = 0
+            for i, (width, v_cols) in enumerate(CHUNKS[pair]):
+                s_cols = width - v_cols
+                src = raw[pair, i][:].rearrange("p t c -> p c t")
+                dst = window[:, 2 * c0 : 2 * (c0 + width)].rearrange("p (c t) -> p c t", t=2)
+                if s_cols:
+                    nc.scalar.copy(dst[:, :s_cols, :], src[:, :s_cols, :])
+                if v_cols:
+                    nc.vector.tensor_copy(dst[:, s_cols:, :], src[:, s_cols:, :])
+                c0 += width
+            return window
+
+        def gather(pair, window, j0, n):
+            z, h = divmod(pair, 2)
+            half, c0 = divmod(j0, HALF)
+            nc.vector.tensor_copy(picked[z, half][:, h, c0 : c0 + n], window[:].bitcast(U32).indirect(entries(j0, n)))
+
+        def weave(z, j0, n, on_scalar):
+            half, c0 = divmod(j0, HALF)
+            woven = keep.tile([P, 4 * n], BF16, name="woven%d_%d" % (z, j0), align_bytes=64)
+            src = picked[z, half][:, :, c0 : c0 + n]
+            if on_scalar:
+                nc.scalar.copy(woven[:].bitcast(U32).rearrange("p (n h) -> p n h", h=2), src.rearrange("p h n -> p n h"))
+            else:
+                nc.vector.tensor_copy(
+                    woven[:].bitcast(I32).rearrange("p (n h) -> p n h", h=2), src.bitcast(I32).rearrange("p h n -> p n h")
+                )
+            return woven
+
+        def quantise(z, j0, n, woven):
+            half, c0 = divmod(j0, HALF)
+            nc.vector.quantize_mx(
+                out=x_codes[z, half][:, c0 : c0 + n].bitcast(FP8X4), scales=x_scale[z, half][:, c0 : c0 + n], in_=woven[:]
+            )
+
+        for pair in range(3):
+            window = cast(pair)
+            for j0 in range(0, S, HALF):
+                gather(pair, window, j0, HALF)
+            if pair == 1:
+                woven = [weave(0, j0, HALF, False) for j0 in range(0, S, HALF)]
+                for half in range(2):
+                    quantise(0, HALF * half, HALF, woven[half])
+        window = cast(3)
+        pieces = list(range(0, S, PIECE))
+        woven = {}
+        for step in range(len(pieces) + 2):
+            if step < len(pieces):
+                gather(3, window, pieces[step], PIECE)
+                woven[step] = weave(1, pieces[step], PIECE, True)
+            if step >= 2:
+                quantise(1, pieces[step - 2], PIECE, woven[step - 2])
+
+        for half in range(2):
+            for b in range(2):
+                acc = []
+                for w in range(2):
+                    bank = psum.tile([P, HALF], F32, name="bank")
+                    for z in range(2):
+                        nc.tensor.matmul_mx(
+                            out=bank[:],
+                            lhsT=w_codes[w][:, z, P * b : P * (b + 1)].bitcast(FP8X4),
+                            lhsT_scale=w_scale[8 * w + 4 * z : P, P * b : P * (b + 1)],
+                            rhs=x_codes[z, half][:].bitcast(FP8X4),
+                            rhs_scale=x_scale[z, half][:],
+                            start=(z == 0),
+                            stop=(z == 1),
+                        )
+                    acc.append(bank)
+                cols = [slice(c0, c0 + PIECE) for c0 in range(0, HALF, PIECE)]
+                y = [work.tile([P, PIECE], F32, name="y") for c in cols]
+                gate = [work.tile([P, PIECE], F32, name="gate") for c in cols]
+                diff = [work.tile([P, PIECE], F32, name="diff") for c in cols]
+                result = [work.tile([P, PIECE], F32, name="result") for c in cols]
+                for i, c in enumerate(cols):
+                    nc.scalar.activation(y[i][:], acc[0][:, c], TANH, bias=zero[:])
+                for i, c in enumerate(cols):
+                    nc.scalar.activation(gate[i][:], acc[1][:, c], TANH, bias=zero[:], scale=0.5)
+                for i, c in enumerate(cols):
+                    nc.vector.tensor_tensor(
+                        diff[i][:], res_rows[b][:].indirect(entries(HALF * half + PIECE * i, PIECE)), y[i][:], ALU.subtract
+                    )
+                for i, c in enumerate(cols):
+                    nc.vector.scalar_tensor_tensor(gate[i][:], gate[i][:], 1.0, diff[i][:], ALU.subtract, ALU.mult)
+                for i, c in enumerate(cols):
+                    nc.vector.scalar_tensor_tensor(result[i][:], gate[i][:], -0.5, y[i][:], ALU.mult, ALU.add)
+                for i, c in enumerate(cols):
+                    j0 = HALF * half + PIECE * i
+                    nc.sync.dma_start(out=out[P * b : P * (b + 1), j0 : j0 + PIECE], in_=result[i][:])

@@ -18,7 +18,8 @@ TANH = mybir.ActivationFunctionType.Tanh
 P = 128
 HALF = 512
 PIECE = 256
-CHUNKS = [[(1024, 0), (1024, 672)], [(1024, 0), (1024, 672)], [(1024, 0), (512, 0), (512, 320)], [(1024, 0), (512, 512), (512, 320)]]
+CHUNKS = [[(1024, 0), (1024, 672)], [(1024, 0), (512, 512), (512, 320)], [(512, 0), (512, 0), (512, 0), (512, 0)], [(512, 0), (512, 0), (512, 256), (256, 256), (256, 128)]]
+UNITS = [(0, 0, 256), (0, 256, 256), (0, 512, 512), (1, 0, 512), (1, 512, 256), (1, 768, 256)]
 
 
 def tile_picked_highway_tanh_l_kernel(
@@ -27,8 +28,7 @@ def tile_picked_highway_tanh_l_kernel(
     nc = tc.nc
     with ExitStack() as ctx:
         keep = ctx.enter_context(tc.tile_pool(name="keep", bufs=1))
-        work = ctx.enter_context(tc.tile_pool(name="work", bufs=4))
-        psum = ctx.enter_context(tc.psum_pool(name="psum", bufs=8))
+        psum = ctx.enter_context(tc.psum_pool(name="psum", bufs=4))
 
         offsets = keep.tile([P, S // 16], U16, name="offsets")
 
@@ -72,13 +72,11 @@ def tile_picked_highway_tanh_l_kernel(
             res_rows.append(rows)
 
         picked = {}
-        x_codes = {}
-        x_scale = {}
         for z in range(2):
             for half in range(2):
                 picked[z, half] = keep.tile([P, 2, HALF], U32, name="picked%d_%d" % (z, half))
-                x_codes[z, half] = keep.tile([P, HALF], U32, name="x_codes%d_%d" % (z, half), align_bytes=64)
-                x_scale[z, half] = keep.tile([P, HALF], U8, name="x_scale%d_%d" % (z, half), align_bytes=64)
+        x_codes = [keep.tile([P, S], U32, name="x_codes%d" % z, align_bytes=64) for z in range(2)]
+        x_scale = [keep.tile([P, S], U8, name="x_scale%d" % z, align_bytes=64) for z in range(2)]
 
         def cast(pair):
             window = keep.tile([P, 2 * T], BF16, name="window%d" % pair)
@@ -112,9 +110,8 @@ def tile_picked_highway_tanh_l_kernel(
             return woven
 
         def quantise(z, j0, n, woven):
-            half, c0 = divmod(j0, HALF)
             nc.vector.quantize_mx(
-                out=x_codes[z, half][:, c0 : c0 + n].bitcast(FP8X4), scales=x_scale[z, half][:, c0 : c0 + n], in_=woven[:]
+                out=x_codes[z][:, j0 : j0 + n].bitcast(FP8X4), scales=x_scale[z][:, j0 : j0 + n], in_=woven[:]
             )
 
         for pair in range(3):
@@ -128,46 +125,56 @@ def tile_picked_highway_tanh_l_kernel(
         window = cast(3)
         pieces = list(range(0, S, PIECE))
         woven = {}
-        for step in range(len(pieces) + 2):
+        for step in range(len(pieces) + 1):
             if step < len(pieces):
                 gather(3, window, pieces[step], PIECE)
                 woven[step] = weave(1, pieces[step], PIECE, True)
-            if step >= 2:
-                quantise(1, pieces[step - 2], PIECE, woven[step - 2])
+            if step >= 1:
+                quantise(1, pieces[step - 1], PIECE, woven[step - 1])
 
-        for half in range(2):
-            for b in range(2):
-                acc = []
-                for w in range(2):
-                    bank = psum.tile([P, HALF], F32, name="bank")
-                    for z in range(2):
-                        nc.tensor.matmul_mx(
-                            out=bank[:],
-                            lhsT=w_codes[w][:, z, P * b : P * (b + 1)].bitcast(FP8X4),
-                            lhsT_scale=w_scale[8 * w + 4 * z : P, P * b : P * (b + 1)],
-                            rhs=x_codes[z, half][:].bitcast(FP8X4),
-                            rhs_scale=x_scale[z, half][:],
-                            start=(z == 0),
-                            stop=(z == 1),
-                        )
-                    acc.append(bank)
-                cols = [slice(c0, c0 + PIECE) for c0 in range(0, HALF, PIECE)]
-                y = [work.tile([P, PIECE], F32, name="y") for c in cols]
-                gate = [work.tile([P, PIECE], F32, name="gate") for c in cols]
-                diff = [work.tile([P, PIECE], F32, name="diff") for c in cols]
-                result = [work.tile([P, PIECE], F32, name="result") for c in cols]
-                for i, c in enumerate(cols):
-                    nc.scalar.activation(y[i][:], acc[0][:, c], TANH, bias=zero[:])
-                for i, c in enumerate(cols):
-                    nc.scalar.activation(gate[i][:], acc[1][:, c], TANH, bias=zero[:], scale=0.5)
-                for i, c in enumerate(cols):
-                    nc.vector.tensor_tensor(
-                        diff[i][:], res_rows[b][:].indirect(entries(HALF * half + PIECE * i, PIECE)), y[i][:], ALU.subtract
+        y = {}
+        gate = {}
+        diff = {}
+
+        def products(u):
+            b, j0, n = UNITS[u]
+            acc = []
+            for w in range(2):
+                bank = psum.tile([P, HALF], F32, name="bank")
+                for z in range(2):
+                    nc.tensor.matmul_mx(
+                        out=bank[:, :n],
+                        lhsT=w_codes[w][:, z, P * b : P * (b + 1)].bitcast(FP8X4),
+                        lhsT_scale=w_scale[8 * w + 4 * z : P, P * b : P * (b + 1)],
+                        rhs=x_codes[z][:, j0 : j0 + n].bitcast(FP8X4),
+                        rhs_scale=x_scale[z][:, j0 : j0 + n],
+                        start=(z == 0),
+                        stop=(z == 1),
                     )
-                for i, c in enumerate(cols):
-                    nc.vector.scalar_tensor_tensor(gate[i][:], gate[i][:], 1.0, diff[i][:], ALU.subtract, ALU.mult)
-                for i, c in enumerate(cols):
-                    nc.vector.scalar_tensor_tensor(result[i][:], gate[i][:], -0.5, y[i][:], ALU.mult, ALU.add)
-                for i, c in enumerate(cols):
-                    j0 = HALF * half + PIECE * i
-                    nc.sync.dma_start(out=out[P * b : P * (b + 1), j0 : j0 + PIECE], in_=result[i][:])
+                acc.append(bank)
+            y[u] = keep.tile([P, n], F32, name="y%d" % u)
+            gate[u] = keep.tile([P, n], F32, name="gate%d" % u)
+            nc.scalar.activation(y[u][:], acc[0][:, :n], TANH, bias=zero[:])
+            nc.scalar.activation(gate[u][:], acc[1][:, :n], TANH, bias=zero[:], scale=0.5)
+
+        def difference(u):
+            b, j0, n = UNITS[u]
+            diff[u] = keep.tile([P, n], F32, name="diff%d" % u)
+            nc.vector.tensor_tensor(diff[u][:], res_rows[b][:].indirect(entries(j0, n)), y[u][:], ALU.subtract)
+
+        def gated(u):
+            nc.vector.scalar_tensor_tensor(gate[u][:], gate[u][:], 1.0, diff[u][:], ALU.subtract, ALU.mult)
+
+        def finish(u):
+            b, j0, n = UNITS[u]
+            nc.vector.scalar_tensor_tensor(diff[u][:], gate[u][:], -0.5, y[u][:], ALU.mult, ALU.add)
+            nc.sync.dma_start(out=out[P * b : P * (b + 1), j0 : j0 + n], in_=diff[u][:])
+
+        for step in range(len(UNITS) + 2):
+            if step < len(UNITS):
+                products(step)
+                difference(step)
+            if 1 <= step <= len(UNITS):
+                gated(step - 1)
+            if step >= 2:
+                finish(step - 2)

@@ -18,7 +18,7 @@ TANH = mybir.ActivationFunctionType.Tanh
 P = 128
 HALF = 512
 PIECE = 256
-CHUNKS = [[(1024, 0), (1024, 672)], [(1024, 0), (512, 512), (512, 320)], [(512, 0), (512, 0), (512, 0), (512, 0)], [(512, 0), (512, 0), (512, 256), (256, 256), (256, 128)]]
+CHUNKS = [[(2048, 1344)], [(2048, 1344)], [(1024, 0), (1024, 256)], [(1024, 0), (512, 512), (512, 320)]]
 UNITS = [(0, 0, 256), (0, 256, 256), (0, 512, 512), (1, 0, 512), (1, 512, 256), (1, 768, 256)]
 
 

@@ -1,6 +1,7 @@
 from contextlib import ExitStack
 
 import concourse.mybir as mybir
+from concourse.masks import make_identity
 
 K, T, S, N = 1024, 2048, 1024, 256
 FLOPS = 2 * 2 * K * N * S
@@ -14,12 +15,13 @@ U8 = mybir.dt.uint8
 FP8X4 = mybir.dt.float8_e4m3fn_x4
 ALU = mybir.AluOpType
 TANH = mybir.ActivationFunctionType.Tanh
+COPY = mybir.ActivationFunctionType.Copy
 
 P = 128
 HALF = 512
 PIECE = 256
-CHUNKS = [[(2048, 1344)], [(2048, 1344)], [(1024, 0), (1024, 256)], [(1024, 0), (512, 512), (512, 320)]]
-UNITS = [(0, 0, 256), (0, 256, 256), (0, 512, 512), (1, 0, 512), (1, 512, 256), (1, 768, 256)]
+CHUNKS = [[(2048, 1344)], [(2048, 1344)], [(1024, 0), (1024, 0)], [(1024, 0), (512, 512), (512, 128)]]
+UNITS = [(0, 512), (512, 256), (768, 256)]
 
 
 def tile_picked_highway_tanh_l_kernel(
@@ -28,7 +30,7 @@ def tile_picked_highway_tanh_l_kernel(
     nc = tc.nc
     with ExitStack() as ctx:
         keep = ctx.enter_context(tc.tile_pool(name="keep", bufs=1))
-        psum = ctx.enter_context(tc.psum_pool(name="psum", bufs=4))
+        psum = ctx.enter_context(tc.psum_pool(name="psum", bufs=8))
 
         offsets = keep.tile([P, S // 16], U16, name="offsets")
 
@@ -40,14 +42,21 @@ def tile_picked_highway_tanh_l_kernel(
         nc.vector.memset(zero_in[:], 0.0)
         nc.scalar.activation(zero[:], zero_in[:], TANH)
 
+        ident = keep.tile([P, P], F32, name="ident")
+        make_identity(nc, ident[:])
+
         w_scale = keep.tile([P, N], U8, name="w_scale", align_bytes=64)
         nc.gpsimd.memset(w_scale[:].bitcast(I32), 0)
-        for w, scales in enumerate((w1_scales, w2_scales)):
-            for q in range(4):
-                nc.gpsimd.dma_start(
-                    out=w_scale[32 * q + 8 * w : 32 * q + 8 * w + 8, :].bitcast(I32),
-                    in_=scales.bitcast(I32)[:, 4 * q : 4 * q + 4, :],
-                )
+
+        def load_scales(queue, w, q):
+            queue.dma_start(
+                out=w_scale[32 * q + 8 * w : 32 * q + 8 * w + 8, :].bitcast(I32),
+                in_=(w1_scales, w2_scales)[w].bitcast(I32)[:, 4 * q : 4 * q + 4, :],
+            )
+
+        for w in range(2):
+            for q in range(3):
+                load_scales(nc.gpsimd, w, q)
 
         x_rows = xT.rearrange("(z p t) c -> z p t c", p=P, t=4)
         raw = {}
@@ -60,6 +69,9 @@ def tile_picked_highway_tanh_l_kernel(
                 if pair == 0 and i == 0:
                     nc.sync.dma_start(offsets[:], offs)
                 c0 += width
+            if pair == 2:
+                for w in range(2):
+                    load_scales(nc.sync, w, 3)
         w_codes = []
         for w, words in enumerate((w1_words, w2_words)):
             codes = keep.tile([P, 2, N], I32, name="w_codes%d" % w, align_bytes=64)
@@ -132,49 +144,146 @@ def tile_picked_highway_tanh_l_kernel(
             if step >= 1:
                 quantise(1, pieces[step - 1], PIECE, woven[step - 1])
 
-        y = {}
-        gate = {}
-        diff = {}
+        def product(w, b, half):
+            bank = psum.tile([P, HALF], F32, name="bank")
+            for z in range(2):
+                nc.tensor.matmul_mx(
+                    out=bank[:],
+                    lhsT=w_codes[w][:, z, P * b : P * (b + 1)].bitcast(FP8X4),
+                    lhsT_scale=w_scale[8 * w + 4 * z : P, P * b : P * (b + 1)],
+                    rhs=x_codes[z][:, HALF * half : HALF * (half + 1)].bitcast(FP8X4),
+                    rhs_scale=x_scale[z][:, HALF * half : HALF * (half + 1)],
+                    start=(z == 0),
+                    stop=(z == 1),
+                )
+            return bank
 
-        def products(u):
-            b, j0, n = UNITS[u]
-            acc = []
-            for w in range(2):
-                bank = psum.tile([P, HALF], F32, name="bank")
+        def turned_gate_product(half):
+            bank = psum.tile([P, HALF], F32, name="bank")
+            for i in range(4):
+                j0 = HALF * half + P * i
                 for z in range(2):
                     nc.tensor.matmul_mx(
-                        out=bank[:, :n],
-                        lhsT=w_codes[w][:, z, P * b : P * (b + 1)].bitcast(FP8X4),
-                        lhsT_scale=w_scale[8 * w + 4 * z : P, P * b : P * (b + 1)],
-                        rhs=x_codes[z][:, j0 : j0 + n].bitcast(FP8X4),
-                        rhs_scale=x_scale[z][:, j0 : j0 + n],
+                        out=bank[:, P * i : P * (i + 1)],
+                        lhsT=x_codes[z][:, j0 : j0 + P].bitcast(FP8X4),
+                        lhsT_scale=x_scale[z][:, j0 : j0 + P],
+                        rhs=w_codes[1][:, z, 0:P].bitcast(FP8X4),
+                        rhs_scale=w_scale[8 + 4 * z : P, 0:P],
                         start=(z == 0),
                         stop=(z == 1),
                     )
-                acc.append(bank)
-            y[u] = keep.tile([P, n], F32, name="y%d" % u)
-            gate[u] = keep.tile([P, n], F32, name="gate%d" % u)
-            nc.scalar.activation(y[u][:], acc[0][:, :n], TANH, bias=zero[:])
-            nc.scalar.activation(gate[u][:], acc[1][:, :n], TANH, bias=zero[:], scale=0.5)
+            return bank
 
-        def difference(u):
-            b, j0, n = UNITS[u]
-            diff[u] = keep.tile([P, n], F32, name="diff%d" % u)
-            nc.vector.tensor_tensor(diff[u][:], res_rows[b][:].indirect(entries(j0, n)), y[u][:], ALU.subtract)
+        acc = {}
+        for half in range(2):
+            acc["y0", half] = product(0, 0, half)
+            acc["y1", half] = product(0, 1, half)
+            acc["g0", half] = turned_gate_product(half)
+            acc["g1", half] = product(1, 1, half)
 
-        def gated(u):
-            nc.vector.scalar_tensor_tensor(gate[u][:], gate[u][:], 1.0, diff[u][:], ALU.subtract, ALU.mult)
+        def turn(bank, src, start, stop):
+            for i in range(4):
+                cols = slice(P * i, P * (i + 1))
+                nc.tensor.matmul(
+                    bank[:, cols], src[:, cols], ident[:], start=start and i == 0, stop=stop and i == 3, is_transpose=True
+                )
 
-        def finish(u):
-            b, j0, n = UNITS[u]
-            nc.vector.scalar_tensor_tensor(diff[u][:], gate[u][:], -0.5, y[u][:], ALU.mult, ALU.add)
-            nc.sync.dma_start(out=out[P * b : P * (b + 1), j0 : j0 + n], in_=diff[u][:])
+        minus_y, gate_t, r0, y_t, e_t, d_bank, f_bank = {}, {}, {}, {}, {}, {}, {}
 
-        for step in range(len(UNITS) + 2):
-            if step < len(UNITS):
-                products(step)
-                difference(step)
-            if 1 <= step <= len(UNITS):
-                gated(step - 1)
-            if step >= 2:
-                finish(step - 2)
+        def a_minus_y(a):
+            minus_y[a] = keep.tile([P, HALF], F32, name="minus_y%d" % a)
+            nc.scalar.activation(minus_y[a][:], acc["y0", a][:], TANH, bias=zero[:], scale=-1.0)
+
+        def a_gate(a):
+            gate_t[a] = keep.tile([P, HALF], F32, name="gate_t%d" % a)
+            nc.scalar.activation(gate_t[a][:], acc["g0", a][:], TANH, bias=zero[:], scale=0.5)
+
+        def a_gather(a):
+            r0[a] = keep.tile([P, HALF], F32, name="r0_%d" % a)
+            nc.vector.tensor_copy(r0[a][:], res_rows[0][:].indirect(entries(HALF * a, HALF)))
+
+        def a_turn_y(a):
+            bank = psum.tile([P, HALF], F32, name="bank")
+            turn(bank, minus_y[a], True, True)
+            y_t[a] = keep.tile([P, HALF], F32, name="y_t%d" % a)
+            nc.scalar.activation(y_t[a][:], bank[:], COPY, scale=2.0)
+
+        def a_diff(a):
+            d_bank[a] = psum.tile([P, HALF], F32, name="bank")
+            turn(d_bank[a], minus_y[a], True, False)
+            turn(d_bank[a], r0[a], False, True)
+
+        def a_gated(a):
+            e_t[a] = keep.tile([P, HALF], F32, name="e_t%d" % a)
+            nc.vector.scalar_tensor_tensor(e_t[a][:], gate_t[a][:], 1.0, d_bank[a][:], ALU.subtract, ALU.mult)
+
+        def a_back_y(a):
+            f_bank[a] = psum.tile([P, HALF], F32, name="bank")
+            turn(f_bank[a], y_t[a], True, False)
+
+        def a_finish(a):
+            turn(f_bank[a], e_t[a], False, True)
+            done = keep.tile([P, HALF], F32, name="done%d" % a)
+            nc.scalar.activation(done[:], f_bank[a][:], COPY, scale=-0.5)
+            nc.sync.dma_start(out=out[0:P, HALF * a : HALF * (a + 1)], in_=done[:])
+
+        y, gate, diff = {}, {}, {}
+
+        def b_y(half):
+            y[half] = keep.tile([P, HALF], F32, name="y%d" % half)
+            nc.scalar.activation(y[half][:], acc["y1", half][:], TANH, bias=zero[:])
+
+        def b_gate(half):
+            gate[half] = keep.tile([P, HALF], F32, name="gate%d" % half)
+            nc.scalar.activation(gate[half][:], acc["g1", half][:], TANH, bias=zero[:], scale=0.5)
+
+        def part(tiles, u):
+            j0, n = UNITS[u]
+            half, c0 = divmod(j0, HALF)
+            return tiles[half][:, c0 : c0 + n]
+
+        def b_diff(u):
+            j0, n = UNITS[u]
+            if u == 0:
+                diff[u] = keep.tile([P, n], F32, name="diff%d" % u)
+            else:
+                diff[u] = part(gate_t, u)
+            nc.vector.tensor_tensor(diff[u][:], res_rows[1][:].indirect(entries(j0, n)), part(y, u), ALU.subtract)
+
+        def b_gated(u):
+            nc.vector.scalar_tensor_tensor(part(gate, u), part(gate, u), 1.0, diff[u][:], ALU.subtract, ALU.mult)
+
+        def b_finish(u):
+            j0, n = UNITS[u]
+            nc.vector.scalar_tensor_tensor(diff[u][:], part(gate, u), -0.5, part(y, u), ALU.mult, ALU.add)
+            nc.sync.dma_start(out=out[P : 2 * P, j0 : j0 + n], in_=diff[u][:])
+
+        a_gather(0)
+        a_gather(1)
+        a_minus_y(0)
+        b_y(0)
+        a_gate(0)
+        a_turn_y(0)
+        a_minus_y(1)
+        a_diff(0)
+        b_diff(0)
+        b_gate(0)
+        a_gate(1)
+        a_back_y(0)
+        a_gated(0)
+        a_turn_y(1)
+        a_diff(1)
+        b_gated(0)
+        b_y(1)
+        b_finish(0)
+        a_back_y(1)
+        a_finish(0)
+        a_gated(1)
+        b_gate(1)
+        b_diff(1)
+        a_finish(1)
+        b_diff(2)
+        b_gated(1)
+        b_gated(2)
+        b_finish(1)
+        b_finish(2)

@@ -20,7 +20,7 @@ COPY = mybir.ActivationFunctionType.Copy
 P = 128
 HALF = 512
 PIECE = 256
-CHUNKS = [[(2048, 1344)], [(2048, 1344)], [(1024, 0), (1024, 0)], [(1024, 0), (512, 512), (512, 128)]]
+CHUNKS = [[(2048, 1344)], [(1024, 0), (1024, 672)], [(1024, 0), (1024, 256)], [(1024, 0), (512, 512), (512, 352)]]
 UNITS = [(0, 512), (512, 256), (768, 256)]
 
 
@@ -144,15 +144,15 @@ def tile_picked_highway_tanh_l_kernel(
             if step >= 1:
                 quantise(1, pieces[step - 1], PIECE, woven[step - 1])
 
-        def product(w, b, half):
+        def product(w, b, j0, n):
             bank = psum.tile([P, HALF], F32, name="bank")
             for z in range(2):
                 nc.tensor.matmul_mx(
-                    out=bank[:],
+                    out=bank[:, :n],
                     lhsT=w_codes[w][:, z, P * b : P * (b + 1)].bitcast(FP8X4),
                     lhsT_scale=w_scale[8 * w + 4 * z : P, P * b : P * (b + 1)],
-                    rhs=x_codes[z][:, HALF * half : HALF * (half + 1)].bitcast(FP8X4),
-                    rhs_scale=x_scale[z][:, HALF * half : HALF * (half + 1)],
+                    rhs=x_codes[z][:, j0 : j0 + n].bitcast(FP8X4),
+                    rhs_scale=x_scale[z][:, j0 : j0 + n],
                     start=(z == 0),
                     stop=(z == 1),
                 )
@@ -175,11 +175,14 @@ def tile_picked_highway_tanh_l_kernel(
             return bank
 
         acc = {}
-        for half in range(2):
-            acc["y0", half] = product(0, 0, half)
-            acc["y1", half] = product(0, 1, half)
-            acc["g0", half] = turned_gate_product(half)
-            acc["g1", half] = product(1, 1, half)
+        acc["first"] = product(0, 0, 0, PIECE)
+        acc["y0", 0] = product(0, 0, PIECE, PIECE)
+        acc["y1", 0] = product(0, 1, 0, HALF)
+        acc["g0", 0] = turned_gate_product(0)
+        acc["g1", 0] = product(1, 1, 0, HALF)
+        acc["y0", 1] = product(0, 0, HALF, HALF)
+        acc["g0", 1] = turned_gate_product(1)
+        acc["y1", 1] = product(0, 1, HALF, HALF)
 
         def turn(bank, src, start, stop):
             for i in range(4):
@@ -192,7 +195,12 @@ def tile_picked_highway_tanh_l_kernel(
 
         def a_minus_y(a):
             minus_y[a] = keep.tile([P, HALF], F32, name="minus_y%d" % a)
-            nc.scalar.activation(minus_y[a][:], acc["y0", a][:], TANH, bias=zero[:], scale=-1.0)
+            if a == 0:
+                nc.scalar.activation(minus_y[a][:, :PIECE], acc["first"][:, :PIECE], TANH, bias=zero[:], scale=-1.0)
+                acc["g1", 1] = product(1, 1, HALF, HALF)
+                nc.scalar.activation(minus_y[a][:, PIECE:], acc["y0", a][:, :PIECE], TANH, bias=zero[:], scale=-1.0)
+            else:
+                nc.scalar.activation(minus_y[a][:], acc["y0", a][:], TANH, bias=zero[:], scale=-1.0)
 
         def a_gate(a):
             gate_t[a] = keep.tile([P, HALF], F32, name="gate_t%d" % a)

@@ -20,6 +20,9 @@ COPY = mybir.ActivationFunctionType.Copy
 P = 128
 HALF = 512
 PIECE = 256
+Y_BANK = [2, 5]
+D_BANK = [1, 3]
+F_BANK = [4, 6]
 CHUNKS = [[(2048, 1344)], [(1024, 0), (1024, 672)], [(1024, 0), (1024, 256)], [(1024, 0), (512, 512), (512, 352)]]
 UNITS = [(0, 512), (512, 256), (768, 256)]
 
@@ -30,7 +33,7 @@ def tile_picked_highway_tanh_l_kernel(
     nc = tc.nc
     with ExitStack() as ctx:
         keep = ctx.enter_context(tc.tile_pool(name="keep", bufs=1))
-        psum = ctx.enter_context(tc.psum_pool(name="psum", bufs=8))
+        psum = ctx.enter_context(tc.psum_pool(name="psum", bufs=1))
 
         offsets = keep.tile([P, S // 16], U16, name="offsets")
 
@@ -144,8 +147,11 @@ def tile_picked_highway_tanh_l_kernel(
             if step >= 1:
                 quantise(1, pieces[step - 1], PIECE, woven[step - 1])
 
-        def product(w, b, j0, n):
-            bank = psum.tile([P, HALF], F32, name="bank")
+        def new_bank(k):
+            return psum.tile([P, HALF], F32, name="bank%d" % k)
+
+        def product(k, w, b, j0, n):
+            bank = new_bank(k)
             for z in range(2):
                 nc.tensor.matmul_mx(
                     out=bank[:, :n],
@@ -158,8 +164,8 @@ def tile_picked_highway_tanh_l_kernel(
                 )
             return bank
 
-        def turned_gate_product(half):
-            bank = psum.tile([P, HALF], F32, name="bank")
+        def turned_gate_product(k, half):
+            bank = new_bank(k)
             for i in range(4):
                 j0 = HALF * half + P * i
                 for z in range(2):
@@ -175,14 +181,14 @@ def tile_picked_highway_tanh_l_kernel(
             return bank
 
         acc = {}
-        acc["first"] = product(0, 0, 0, PIECE)
-        acc["y0", 0] = product(0, 0, PIECE, PIECE)
-        acc["y1", 0] = product(0, 1, 0, HALF)
-        acc["g0", 0] = turned_gate_product(0)
-        acc["g1", 0] = product(1, 1, 0, HALF)
-        acc["y0", 1] = product(0, 0, HALF, HALF)
-        acc["g0", 1] = turned_gate_product(1)
-        acc["y1", 1] = product(0, 1, HALF, HALF)
+        acc["first"] = product(0, 0, 0, 0, PIECE)
+        acc["y0", 0] = product(1, 0, 0, PIECE, PIECE)
+        acc["y1", 0] = product(2, 0, 1, 0, HALF)
+        acc["g0", 0] = turned_gate_product(3, 0)
+        acc["g1", 0] = product(4, 1, 1, 0, HALF)
+        acc["g0", 1] = turned_gate_product(5, 1)
+        acc["y0", 1] = product(6, 0, 0, HALF, HALF)
+        acc["y1", 1] = product(7, 0, 1, HALF, HALF)
 
         def turn(bank, src, start, stop):
             for i in range(4):
@@ -191,13 +197,14 @@ def tile_picked_highway_tanh_l_kernel(
                     bank[:, cols], src[:, cols], ident[:], start=start and i == 0, stop=stop and i == 3, is_transpose=True
                 )
 
+        stored = {}
         minus_y, gate_t, r0, y_t, e_t, d_bank, f_bank = {}, {}, {}, {}, {}, {}, {}
 
         def a_minus_y(a):
             minus_y[a] = keep.tile([P, HALF], F32, name="minus_y%d" % a)
             if a == 0:
                 nc.scalar.activation(minus_y[a][:, :PIECE], acc["first"][:, :PIECE], TANH, bias=zero[:], scale=-1.0)
-                acc["g1", 1] = product(1, 1, HALF, HALF)
+                acc["g1", 1] = product(0, 1, 1, HALF, HALF)
                 nc.scalar.activation(minus_y[a][:, PIECE:], acc["y0", a][:, :PIECE], TANH, bias=zero[:], scale=-1.0)
             else:
                 nc.scalar.activation(minus_y[a][:], acc["y0", a][:], TANH, bias=zero[:], scale=-1.0)
@@ -211,29 +218,32 @@ def tile_picked_highway_tanh_l_kernel(
             nc.vector.tensor_copy(r0[a][:], res_rows[0][:].indirect(entries(HALF * a, HALF)))
 
         def a_turn_y(a):
-            bank = psum.tile([P, HALF], F32, name="bank")
-            turn(bank, minus_y[a], True, True)
+            bank = new_bank(Y_BANK[a])
+            turn(bank, r0[a], True, True)
             y_t[a] = keep.tile([P, HALF], F32, name="y_t%d" % a)
-            nc.scalar.activation(y_t[a][:], bank[:], COPY, scale=2.0)
+            nc.scalar.activation(y_t[a][:], bank[:], COPY, scale=-2.0)
 
         def a_diff(a):
-            d_bank[a] = psum.tile([P, HALF], F32, name="bank")
+            d_bank[a] = new_bank(D_BANK[a])
             turn(d_bank[a], minus_y[a], True, False)
             turn(d_bank[a], r0[a], False, True)
 
         def a_gated(a):
             e_t[a] = keep.tile([P, HALF], F32, name="e_t%d" % a)
-            nc.vector.scalar_tensor_tensor(e_t[a][:], gate_t[a][:], 1.0, d_bank[a][:], ALU.subtract, ALU.mult)
+            nc.vector.scalar_tensor_tensor(e_t[a][:], gate_t[a][:], 1.0, d_bank[a][:], ALU.add, ALU.mult)
 
         def a_back_y(a):
-            f_bank[a] = psum.tile([P, HALF], F32, name="bank")
+            f_bank[a] = new_bank(F_BANK[a])
             turn(f_bank[a], y_t[a], True, False)
 
         def a_finish(a):
             turn(f_bank[a], e_t[a], False, True)
             done = keep.tile([P, HALF], F32, name="done%d" % a)
-            nc.scalar.activation(done[:], f_bank[a][:], COPY, scale=-0.5)
-            nc.sync.dma_start(out=out[0:P, HALF * a : HALF * (a + 1)], in_=done[:])
+            stored[a] = done
+            n = HALF
+            for c0 in range(0, HALF, n):
+                nc.scalar.activation(done[:, c0 : c0 + n], f_bank[a][:, c0 : c0 + n], COPY, scale=-0.5)
+                nc.scalar.dma_start(out=out[0:P, HALF * a + c0 : HALF * a + c0 + n], in_=done[:, c0 : c0 + n])
 
         y, gate, diff = {}, {}, {}
 
@@ -263,30 +273,31 @@ def tile_picked_highway_tanh_l_kernel(
 
         def b_finish(u):
             j0, n = UNITS[u]
-            nc.vector.scalar_tensor_tensor(diff[u][:], part(gate, u), -0.5, part(y, u), ALU.mult, ALU.add)
-            nc.sync.dma_start(out=out[P : 2 * P, j0 : j0 + n], in_=diff[u][:])
+            done = r0[1][:] if u == 0 else diff[u][:]
+            nc.vector.scalar_tensor_tensor(done, part(gate, u), -0.5, part(y, u), ALU.mult, ALU.add)
+            nc.sync.dma_start(out=out[P : 2 * P, j0 : j0 + n], in_=done)
 
         a_gather(0)
         a_gather(1)
         a_minus_y(0)
         b_y(0)
         a_gate(0)
-        a_turn_y(0)
+        a_gate(1)
         a_minus_y(1)
         a_diff(0)
+        a_turn_y(0)
+        a_diff(1)
         b_diff(0)
         b_gate(0)
-        a_gate(1)
+        a_turn_y(1)
         a_back_y(0)
         a_gated(0)
-        a_turn_y(1)
-        a_diff(1)
         b_gated(0)
         b_y(1)
-        b_finish(0)
         a_back_y(1)
-        a_finish(0)
         a_gated(1)
+        b_finish(0)
+        a_finish(0)
         b_gate(1)
         b_diff(1)
         a_finish(1)

@@ -20,9 +20,9 @@ COPY = mybir.ActivationFunctionType.Copy
 P = 128
 HALF = 512
 PIECE = 256
-Y_BANK = [2, 5]
-D_BANK = [1, 3]
-F_BANK = [4, 6]
+Y_BANK = [6, 4]
+D_BANK = [5, 3]
+F_BANK = [0, 1]
 CHUNKS = [[(2048, 1344)], [(1024, 0), (1024, 672)], [(1024, 0), (1024, 256)], [(1024, 0), (512, 512), (512, 352)]]
 UNITS = [(0, 512), (512, 256), (768, 256)]
 
@@ -185,9 +185,9 @@ def tile_picked_highway_tanh_l_kernel(
         acc["y0", 0] = product(1, 0, 0, PIECE, PIECE)
         acc["y1", 0] = product(2, 0, 1, 0, HALF)
         acc["g0", 0] = turned_gate_product(3, 0)
-        acc["g1", 0] = product(4, 1, 1, 0, HALF)
         acc["g0", 1] = turned_gate_product(5, 1)
         acc["y0", 1] = product(6, 0, 0, HALF, HALF)
+        acc["g1", 0] = product(4, 1, 1, 0, HALF)
         acc["y1", 1] = product(7, 0, 1, HALF, HALF)
 
         def turn(bank, src, start, stop):
@@ -204,7 +204,6 @@ def tile_picked_highway_tanh_l_kernel(
             minus_y[a] = keep.tile([P, HALF], F32, name="minus_y%d" % a)
             if a == 0:
                 nc.scalar.activation(minus_y[a][:, :PIECE], acc["first"][:, :PIECE], TANH, bias=zero[:], scale=-1.0)
-                acc["g1", 1] = product(0, 1, 1, HALF, HALF)
                 nc.scalar.activation(minus_y[a][:, PIECE:], acc["y0", a][:, :PIECE], TANH, bias=zero[:], scale=-1.0)
             else:
                 nc.scalar.activation(minus_y[a][:], acc["y0", a][:], TANH, bias=zero[:], scale=-1.0)
@@ -273,7 +272,7 @@ def tile_picked_highway_tanh_l_kernel(
 
         def b_finish(u):
             j0, n = UNITS[u]
-            done = r0[1][:] if u == 0 else diff[u][:]
+            done = diff[u][:]
             nc.vector.scalar_tensor_tensor(done, part(gate, u), -0.5, part(y, u), ALU.mult, ALU.add)
             nc.sync.dma_start(out=out[P : 2 * P, j0 : j0 + n], in_=done)
 
@@ -284,21 +283,22 @@ def tile_picked_highway_tanh_l_kernel(
         a_gate(0)
         a_gate(1)
         a_minus_y(1)
-        a_diff(0)
-        a_turn_y(0)
-        a_diff(1)
-        b_diff(0)
         b_gate(0)
+        b_y(1)
+        a_diff(0)
+        a_diff(1)
+        a_turn_y(0)
         a_turn_y(1)
+        acc["g1", 1] = product(7, 1, 1, HALF, HALF)
+        b_diff(0)
         a_back_y(0)
         a_gated(0)
         b_gated(0)
-        b_y(1)
         a_back_y(1)
         a_gated(1)
         b_finish(0)
-        a_finish(0)
         b_gate(1)
+        a_finish(0)
         b_diff(1)
         a_finish(1)
         b_diff(2)

@@ -19,12 +19,16 @@ COPY = mybir.ActivationFunctionType.Copy
 
 P = 128
 HALF = 512
-PIECE = 256
-Y_BANK = [6, 4]
-D_BANK = [5, 3]
-F_BANK = [0, 1]
-CHUNKS = [[(2048, 1344)], [(1024, 0), (1024, 672)], [(1024, 0), (1024, 256)], [(1024, 0), (512, 512), (512, 352)]]
-UNITS = [(0, 512), (512, 256), (768, 256)]
+QUARTER = 256
+
+LOADS = [
+    [(2048, 1344)],
+    [(1024, 0), (1024, 672)],
+    [(1024, 0), (1024, 256)],
+    [(768, 0), (768, 352), (512, 352)],
+]
+
+STRETCHES = [(0, HALF), (HALF, QUARTER), (HALF + QUARTER, QUARTER)]
 
 
 def tile_picked_highway_tanh_l_kernel(
@@ -66,10 +70,10 @@ def tile_picked_highway_tanh_l_kernel(
         for pair in range(4):
             z, h = divmod(pair, 2)
             c0 = 0
-            for i, (width, v_cols) in enumerate(CHUNKS[pair]):
-                raw[pair, i] = keep.tile([P, 2, width], F32, name="raw%d_%d" % (pair, i))
-                nc.sync.dma_start(out=raw[pair, i][:], in_=x_rows[z, :, 2 * h : 2 * h + 2, c0 : c0 + width])
-                if pair == 0 and i == 0:
+            for load, (width, v_cols) in enumerate(LOADS[pair]):
+                raw[pair, load] = keep.tile([P, 2, width], F32, name="raw%d_%d" % (pair, load))
+                nc.sync.dma_start(out=raw[pair, load][:], in_=x_rows[z, :, 2 * h : 2 * h + 2, c0 : c0 + width])
+                if pair == 0:
                     nc.sync.dma_start(offsets[:], offs)
                 c0 += width
             if pair == 2:
@@ -93,12 +97,12 @@ def tile_picked_highway_tanh_l_kernel(
         x_codes = [keep.tile([P, S], U32, name="x_codes%d" % z, align_bytes=64) for z in range(2)]
         x_scale = [keep.tile([P, S], U8, name="x_scale%d" % z, align_bytes=64) for z in range(2)]
 
-        def cast(pair):
+        def round_pair(pair):
             window = keep.tile([P, 2 * T], BF16, name="window%d" % pair)
             c0 = 0
-            for i, (width, v_cols) in enumerate(CHUNKS[pair]):
+            for load, (width, v_cols) in enumerate(LOADS[pair]):
                 s_cols = width - v_cols
-                src = raw[pair, i][:].rearrange("p t c -> p c t")
+                src = raw[pair, load][:].rearrange("p t c -> p c t")
                 dst = window[:, 2 * c0 : 2 * (c0 + width)].rearrange("p (c t) -> p c t", t=2)
                 if s_cols:
                     nc.scalar.copy(dst[:, :s_cols, :], src[:, :s_cols, :])
@@ -107,16 +111,16 @@ def tile_picked_highway_tanh_l_kernel(
                 c0 += width
             return window
 
-        def gather(pair, window, j0, n):
+        def gather_pair(pair, window, j0, n):
             z, h = divmod(pair, 2)
             half, c0 = divmod(j0, HALF)
             nc.vector.tensor_copy(picked[z, half][:, h, c0 : c0 + n], window[:].bitcast(U32).indirect(entries(j0, n)))
 
-        def weave(z, j0, n, on_scalar):
+        def weave(z, j0, n):
             half, c0 = divmod(j0, HALF)
             woven = keep.tile([P, 4 * n], BF16, name="woven%d_%d" % (z, j0), align_bytes=64)
             src = picked[z, half][:, :, c0 : c0 + n]
-            if on_scalar:
+            if z == 1:
                 nc.scalar.copy(woven[:].bitcast(U32).rearrange("p (n h) -> p n h", h=2), src.rearrange("p h n -> p n h"))
             else:
                 nc.vector.tensor_copy(
@@ -130,28 +134,28 @@ def tile_picked_highway_tanh_l_kernel(
             )
 
         for pair in range(3):
-            window = cast(pair)
+            window = round_pair(pair)
             for j0 in range(0, S, HALF):
-                gather(pair, window, j0, HALF)
+                gather_pair(pair, window, j0, HALF)
             if pair == 1:
-                woven = [weave(0, j0, HALF, False) for j0 in range(0, S, HALF)]
+                woven_halves = [weave(0, j0, HALF) for j0 in range(0, S, HALF)]
                 for half in range(2):
-                    quantise(0, HALF * half, HALF, woven[half])
-        window = cast(3)
-        pieces = list(range(0, S, PIECE))
-        woven = {}
-        for step in range(len(pieces) + 1):
-            if step < len(pieces):
-                gather(3, window, pieces[step], PIECE)
-                woven[step] = weave(1, pieces[step], PIECE, True)
+                    quantise(0, HALF * half, HALF, woven_halves[half])
+
+        window = round_pair(3)
+        woven_quarters = []
+        for step in range(S // QUARTER + 1):
+            if step < S // QUARTER:
+                gather_pair(3, window, QUARTER * step, QUARTER)
+                woven_quarters.append(weave(1, QUARTER * step, QUARTER))
             if step >= 1:
-                quantise(1, pieces[step - 1], PIECE, woven[step - 1])
+                quantise(1, QUARTER * (step - 1), QUARTER, woven_quarters[step - 1])
 
-        def new_bank(k):
-            return psum.tile([P, HALF], F32, name="bank%d" % k)
+        def new_bank(number):
+            return psum.tile([P, HALF], F32, name="bank%d" % number)
 
-        def product(k, w, b, j0, n):
-            bank = new_bank(k)
+        def product(number, w, b, j0, n):
+            bank = new_bank(number)
             for z in range(2):
                 nc.tensor.matmul_mx(
                     out=bank[:, :n],
@@ -164,9 +168,9 @@ def tile_picked_highway_tanh_l_kernel(
                 )
             return bank
 
-        def turned_gate_product(k, half):
-            bank = new_bank(k)
-            for i in range(4):
+        def turned_gate_product(number, half):
+            bank = new_bank(number)
+            for i in range(HALF // P):
                 j0 = HALF * half + P * i
                 for z in range(2):
                     nc.tensor.matmul_mx(
@@ -180,129 +184,111 @@ def tile_picked_highway_tanh_l_kernel(
                     )
             return bank
 
-        acc = {}
-        acc["first"] = product(0, 0, 0, 0, PIECE)
-        acc["y0", 0] = product(1, 0, 0, PIECE, PIECE)
-        acc["y1", 0] = product(2, 0, 1, 0, HALF)
-        acc["g0", 0] = turned_gate_product(3, 0)
-        acc["g0", 1] = turned_gate_product(5, 1)
-        acc["y0", 1] = product(6, 0, 0, HALF, HALF)
-        acc["g1", 0] = product(4, 1, 1, 0, HALF)
-        acc["y1", 1] = product(7, 0, 1, HALF, HALF)
-
         def turn(bank, src, start, stop):
-            for i in range(4):
+            last = HALF // P - 1
+            for i in range(HALF // P):
                 cols = slice(P * i, P * (i + 1))
                 nc.tensor.matmul(
-                    bank[:, cols], src[:, cols], ident[:], start=start and i == 0, stop=stop and i == 3, is_transpose=True
+                    bank[:, cols], src[:, cols], ident[:], start=start and i == 0, stop=stop and i == last, is_transpose=True
                 )
 
-        stored = {}
-        minus_y, gate_t, r0, y_t, e_t, d_bank, f_bank = {}, {}, {}, {}, {}, {}, {}
+        def new_tile(name, half):
+            return keep.tile([P, HALF], F32, name="%s%d" % (name, half))
 
-        def a_minus_y(a):
-            minus_y[a] = keep.tile([P, HALF], F32, name="minus_y%d" % a)
-            if a == 0:
-                nc.scalar.activation(minus_y[a][:, :PIECE], acc["first"][:, :PIECE], TANH, bias=zero[:], scale=-1.0)
-                nc.scalar.activation(minus_y[a][:, PIECE:], acc["y0", a][:, :PIECE], TANH, bias=zero[:], scale=-1.0)
-            else:
-                nc.scalar.activation(minus_y[a][:], acc["y0", a][:], TANH, bias=zero[:], scale=-1.0)
+        def tanh(dst, src, scale):
+            nc.scalar.activation(dst, src, TANH, bias=zero[:], scale=scale)
 
-        def a_gate(a):
-            gate_t[a] = keep.tile([P, HALF], F32, name="gate_t%d" % a)
-            nc.scalar.activation(gate_t[a][:], acc["g0", a][:], TANH, bias=zero[:], scale=0.5)
+        u_y0_quarters = [product(quarter, 0, 0, QUARTER * quarter, QUARTER) for quarter in range(2)]
+        u_y1_first = product(2, 0, 1, 0, HALF)
+        u_gate0_first = turned_gate_product(3, 0)
+        u_gate0_second = turned_gate_product(5, 1)
+        u_y0_second = product(6, 0, 0, HALF, HALF)
+        u_gate1_first = product(4, 1, 1, 0, HALF)
+        u_y1_second = product(7, 0, 1, HALF, HALF)
 
-        def a_gather(a):
-            r0[a] = keep.tile([P, HALF], F32, name="r0_%d" % a)
-            nc.vector.tensor_copy(r0[a][:], res_rows[0][:].indirect(entries(HALF * a, HALF)))
+        r0 = []
+        for half in range(2):
+            r0.append(new_tile("r0_", half))
+            nc.vector.tensor_copy(r0[half][:], res_rows[0][:].indirect(entries(HALF * half, HALF)))
 
-        def a_turn_y(a):
-            bank = new_bank(Y_BANK[a])
-            turn(bank, r0[a], True, True)
-            y_t[a] = keep.tile([P, HALF], F32, name="y_t%d" % a)
-            nc.scalar.activation(y_t[a][:], bank[:], COPY, scale=-2.0)
+        minus_y0, s0, y1, s1 = {}, {}, {}, {}
+        minus_y0[0] = new_tile("minus_y0_", 0)
+        for quarter, bank in enumerate(u_y0_quarters):
+            tanh(minus_y0[0][:, QUARTER * quarter : QUARTER * (quarter + 1)], bank[:, :QUARTER], -1.0)
+        y1[0] = new_tile("y1_", 0)
+        tanh(y1[0][:], u_y1_first[:], 1.0)
+        for half, bank in enumerate((u_gate0_first, u_gate0_second)):
+            s0[half] = new_tile("s0_", half)
+            tanh(s0[half][:], bank[:], 0.5)
+        minus_y0[1] = new_tile("minus_y0_", 1)
+        tanh(minus_y0[1][:], u_y0_second[:], -1.0)
+        s1[0] = new_tile("s1_", 0)
+        tanh(s1[0][:], u_gate1_first[:], 0.5)
+        y1[1] = new_tile("y1_", 1)
+        tanh(y1[1][:], u_y1_second[:], 1.0)
 
-        def a_diff(a):
-            d_bank[a] = new_bank(D_BANK[a])
-            turn(d_bank[a], minus_y[a], True, False)
-            turn(d_bank[a], r0[a], False, True)
+        d0 = []
+        for half, number in enumerate((5, 3)):
+            d0.append(new_bank(number))
+            turn(d0[half], minus_y0[half], True, False)
+            turn(d0[half], r0[half], False, True)
+        minus_2r0 = []
+        for half, number in enumerate((6, 4)):
+            bank = new_bank(number)
+            turn(bank, r0[half], True, True)
+            minus_2r0.append(new_tile("minus_2r0_", half))
+            nc.scalar.activation(minus_2r0[half][:], bank[:], COPY, scale=-2.0)
 
-        def a_gated(a):
-            e_t[a] = keep.tile([P, HALF], F32, name="e_t%d" % a)
-            nc.vector.scalar_tensor_tensor(e_t[a][:], gate_t[a][:], 1.0, d_bank[a][:], ALU.add, ALU.mult)
+        u_gate1_second = product(7, 1, 1, HALF, HALF)
 
-        def a_back_y(a):
-            f_bank[a] = new_bank(F_BANK[a])
-            turn(f_bank[a], y_t[a], True, False)
+        e0, sum0, d1 = {}, {}, {}
 
-        def a_finish(a):
-            turn(f_bank[a], e_t[a], False, True)
-            done = keep.tile([P, HALF], F32, name="done%d" % a)
-            stored[a] = done
-            n = HALF
-            for c0 in range(0, HALF, n):
-                nc.scalar.activation(done[:, c0 : c0 + n], f_bank[a][:, c0 : c0 + n], COPY, scale=-0.5)
-                nc.scalar.dma_start(out=out[0:P, HALF * a + c0 : HALF * a + c0 + n], in_=done[:, c0 : c0 + n])
+        def open_sum0(half):
+            sum0[half] = new_bank(half)
+            turn(sum0[half], minus_2r0[half], True, False)
 
-        y, gate, diff = {}, {}, {}
+        def multiply0(half):
+            e0[half] = new_tile("e0_", half)
+            nc.vector.scalar_tensor_tensor(e0[half][:], s0[half][:], 1.0, d0[half][:], ALU.add, ALU.mult)
 
-        def b_y(half):
-            y[half] = keep.tile([P, HALF], F32, name="y%d" % half)
-            nc.scalar.activation(y[half][:], acc["y1", half][:], TANH, bias=zero[:])
+        def finish0(half):
+            turn(sum0[half], e0[half], False, True)
+            out0 = new_tile("out0_", half)
+            nc.scalar.activation(out0[:], sum0[half][:], COPY, scale=-0.5)
+            nc.scalar.dma_start(out=out[0:P, HALF * half : HALF * (half + 1)], in_=out0[:])
 
-        def b_gate(half):
-            gate[half] = keep.tile([P, HALF], F32, name="gate%d" % half)
-            nc.scalar.activation(gate[half][:], acc["g1", half][:], TANH, bias=zero[:], scale=0.5)
-
-        def part(tiles, u):
-            j0, n = UNITS[u]
+        def stretch(tiles, nr):
+            j0, n = STRETCHES[nr]
             half, c0 = divmod(j0, HALF)
             return tiles[half][:, c0 : c0 + n]
 
-        def b_diff(u):
-            j0, n = UNITS[u]
-            if u == 0:
-                diff[u] = keep.tile([P, n], F32, name="diff%d" % u)
-            else:
-                diff[u] = part(gate_t, u)
-            nc.vector.tensor_tensor(diff[u][:], res_rows[1][:].indirect(entries(j0, n)), part(y, u), ALU.subtract)
+        def subtract1(nr, dst):
+            j0, n = STRETCHES[nr]
+            d1[nr] = dst
+            nc.vector.tensor_tensor(dst, res_rows[1][:].indirect(entries(j0, n)), stretch(y1, nr), ALU.subtract)
 
-        def b_gated(u):
-            nc.vector.scalar_tensor_tensor(part(gate, u), part(gate, u), 1.0, diff[u][:], ALU.subtract, ALU.mult)
+        def multiply1(nr):
+            nc.vector.scalar_tensor_tensor(stretch(s1, nr), stretch(s1, nr), 1.0, d1[nr], ALU.subtract, ALU.mult)
 
-        def b_finish(u):
-            j0, n = UNITS[u]
-            done = diff[u][:]
-            nc.vector.scalar_tensor_tensor(done, part(gate, u), -0.5, part(y, u), ALU.mult, ALU.add)
-            nc.sync.dma_start(out=out[P : 2 * P, j0 : j0 + n], in_=done)
+        def finish1(nr):
+            j0, n = STRETCHES[nr]
+            nc.vector.scalar_tensor_tensor(d1[nr], stretch(s1, nr), -0.5, stretch(y1, nr), ALU.mult, ALU.add)
+            nc.sync.dma_start(out=out[P : 2 * P, j0 : j0 + n], in_=d1[nr])
 
-        a_gather(0)
-        a_gather(1)
-        a_minus_y(0)
-        b_y(0)
-        a_gate(0)
-        a_gate(1)
-        a_minus_y(1)
-        b_gate(0)
-        b_y(1)
-        a_diff(0)
-        a_diff(1)
-        a_turn_y(0)
-        a_turn_y(1)
-        acc["g1", 1] = product(7, 1, 1, HALF, HALF)
-        b_diff(0)
-        a_back_y(0)
-        a_gated(0)
-        b_gated(0)
-        a_back_y(1)
-        a_gated(1)
-        b_finish(0)
-        b_gate(1)
-        a_finish(0)
-        b_diff(1)
-        a_finish(1)
-        b_diff(2)
-        b_gated(1)
-        b_gated(2)
-        b_finish(1)
-        b_finish(2)
+        d1_first = new_tile("d1_", 0)
+        subtract1(0, d1_first[:])
+        open_sum0(0)
+        multiply0(0)
+        multiply1(0)
+        open_sum0(1)
+        multiply0(1)
+        finish1(0)
+        s1[1] = new_tile("s1_", 1)
+        tanh(s1[1][:], u_gate1_second[:], 0.5)
+
+        for nr in (1, 2):
+            finish0(nr - 1)
+            subtract1(nr, stretch(s0, nr))
+        for stage in (multiply1, finish1):
+            for nr in (1, 2):
+                stage(nr)

@@ -25,7 +25,7 @@ LOADS = [
     [(2048, 1344)],
     [(1024, 0), (1024, 672)],
     [(1024, 0), (1024, 256)],
-    [(768, 0), (768, 352), (512, 352)],
+    [(768, 0), (768, 352), (512, 288)],
 ]
 
 STRETCHES = [(0, HALF), (HALF, QUARTER), (HALF + QUARTER, QUARTER)]
@@ -52,18 +52,13 @@ def tile_picked_highway_tanh_l_kernel(
         ident = keep.tile([P, P], F32, name="ident")
         make_identity(nc, ident[:])
 
-        w_scale = keep.tile([P, N], U8, name="w_scale", align_bytes=64)
-        nc.gpsimd.memset(w_scale[:].bitcast(I32), 0)
+        w_scale = keep.tile([P, 4 * N], U8, name="w_scale", align_bytes=64)
+        scale_words = w_scale[:].bitcast(I32)
+        nc.gpsimd.memset(scale_words, 0)
 
-        def load_scales(queue, w, q):
-            queue.dma_start(
-                out=w_scale[32 * q + 8 * w : 32 * q + 8 * w + 8, :].bitcast(I32),
-                in_=(w1_scales, w2_scales)[w].bitcast(I32)[:, 4 * q : 4 * q + 4, :],
-            )
-
-        for w in range(2):
-            for q in range(3):
-                load_scales(nc.gpsimd, w, q)
+        def scale_plane(w, z, b):
+            c0 = N * (2 * w + z) + P * b
+            return w_scale[:, c0 : c0 + P]
 
         x_rows = xT.rearrange("(z p t) c -> z p t c", p=P, t=4)
         raw = {}
@@ -75,10 +70,15 @@ def tile_picked_highway_tanh_l_kernel(
                 nc.sync.dma_start(out=raw[pair, load][:], in_=x_rows[z, :, 2 * h : 2 * h + 2, c0 : c0 + width])
                 if pair == 0:
                     nc.sync.dma_start(offsets[:], offs)
+                    for w, scales in enumerate((w1_scales, w2_scales)):
+                        nc.sync.dma_start(
+                            out=scale_words[0:16, N // 2 * w : N // 2 * (w + 1)].rearrange("r (z n) -> r z n", z=2),
+                            in_=scales.bitcast(I32).rearrange("z r n -> r z n"),
+                        )
                 c0 += width
             if pair == 2:
-                for w in range(2):
-                    load_scales(nc.sync, w, 3)
+                for q in range(1, 4):
+                    nc.sync.dma_start(out=scale_words[32 * q : 32 * q + 4, :], in_=scale_words[4 * q : 4 * q + 4, :])
         w_codes = []
         for w, words in enumerate((w1_words, w2_words)):
             codes = keep.tile([P, 2, N], I32, name="w_codes%d" % w, align_bytes=64)
@@ -160,7 +160,7 @@ def tile_picked_highway_tanh_l_kernel(
                 nc.tensor.matmul_mx(
                     out=bank[:, :n],
                     lhsT=w_codes[w][:, z, P * b : P * (b + 1)].bitcast(FP8X4),
-                    lhsT_scale=w_scale[8 * w + 4 * z : P, P * b : P * (b + 1)],
+                    lhsT_scale=scale_plane(w, z, b),
                     rhs=x_codes[z][:, j0 : j0 + n].bitcast(FP8X4),
                     rhs_scale=x_scale[z][:, j0 : j0 + n],
                     start=(z == 0),
@@ -178,7 +178,7 @@ def tile_picked_highway_tanh_l_kernel(
                         lhsT=x_codes[z][:, j0 : j0 + P].bitcast(FP8X4),
                         lhsT_scale=x_scale[z][:, j0 : j0 + P],
                         rhs=w_codes[1][:, z, 0:P].bitcast(FP8X4),
-                        rhs_scale=w_scale[8 + 4 * z : P, 0:P],
+                        rhs_scale=scale_plane(1, z, 0),
                         start=(z == 0),
                         stop=(z == 1),
                     )

@@ -233,7 +233,7 @@ def tile_picked_highway_tanh_l_kernel(
             turn(d0[half], minus_y0[half], True, False)
             turn(d0[half], r0[half], False, True)
         minus_2r0 = []
-        for half, number in enumerate((6, 4)):
+        for half, number in enumerate((2, 6)):
             bank = new_bank(number)
             turn(bank, r0[half], True, True)
             minus_2r0.append(new_tile("minus_2r0_", half))

@@ -1,7 +1,6 @@
 from contextlib import ExitStack
 
 import concourse.mybir as mybir
-from concourse.masks import make_identity
 
 K, T, S, N = 1024, 2048, 1024, 256
 FLOPS = 2 * 2 * K * N * S
@@ -21,15 +20,6 @@ P = 128
 HALF = 512
 QUARTER = 256
 
-LOADS = [
-    [(2048, 1344)],
-    [(1024, 0), (1024, 672)],
-    [(1024, 0), (1024, 256)],
-    [(768, 0), (768, 352), (512, 288)],
-]
-
-STRETCHES = [(0, HALF), (HALF, QUARTER), (HALF + QUARTER, QUARTER)]
-
 
 def tile_picked_highway_tanh_l_kernel(
     tc, xT, res, w1_words, w1_scales, w2_words, w2_scales, offs, out
@@ -44,153 +34,115 @@ def tile_picked_highway_tanh_l_kernel(
         def entries(j0, n):
             return offsets[:, j0 // 16 : (j0 + n) // 16]
 
+        staged = []
+        for w, scales in enumerate((w1_scales, w2_scales)):
+            rows = keep.tile([4, 2, 4, N // 4], I32, name="staged%d" % w)
+            nc.scalar.dma_start(
+                out=rows[:].rearrange("r z q n -> r (z q) n"),
+                in_=scales.bitcast(I32).rearrange("z (q r) n -> r (z q) n", r=4),
+            )
+            staged.append(rows)
+
         zero_in = keep.tile([P, 1], F32, name="zero_in")
         zero = keep.tile([P, 1], F32, name="zero")
         nc.vector.memset(zero_in[:], 0.0)
         nc.scalar.activation(zero[:], zero_in[:], TANH)
 
-        ident = keep.tile([P, P], F32, name="ident")
-        make_identity(nc, ident[:])
+        w_scale = []
+        for w in range(2):
+            w_scale.append(keep.tile([P, 2, N], U8, name="w_scale%d" % w, align_bytes=64))
+            nc.gpsimd.memset(w_scale[w][:].bitcast(I32), 0)
 
-        w_scale = keep.tile([P, 4 * N], U8, name="w_scale", align_bytes=64)
-        scale_words = w_scale[:].bitcast(I32)
-        nc.gpsimd.memset(scale_words, 0)
-
-        def scale_plane(w, z, b):
-            c0 = N * (2 * w + z) + P * b
-            return w_scale[:, c0 : c0 + P]
-
-        x_rows = xT.rearrange("(z p t) c -> z p t c", p=P, t=4)
-        raw = {}
-        for pair in range(4):
-            z, h = divmod(pair, 2)
-            c0 = 0
-            for load, (width, v_cols) in enumerate(LOADS[pair]):
-                raw[pair, load] = keep.tile([P, 2, width], F32, name="raw%d_%d" % (pair, load))
-                nc.sync.dma_start(out=raw[pair, load][:], in_=x_rows[z, :, 2 * h : 2 * h + 2, c0 : c0 + width])
-                if pair == 0:
-                    nc.sync.dma_start(offsets[:], offs)
-                    for w, scales in enumerate((w1_scales, w2_scales)):
-                        nc.sync.dma_start(
-                            out=scale_words[0:16, N // 2 * w : N // 2 * (w + 1)].rearrange("r (z n) -> r z n", z=2),
-                            in_=scales.bitcast(I32).rearrange("z r n -> r z n"),
-                        )
-                c0 += width
-            if pair == 2:
-                for q in range(1, 4):
-                    nc.sync.dma_start(out=scale_words[32 * q : 32 * q + 4, :], in_=scale_words[4 * q : 4 * q + 4, :])
-        w_codes = []
-        for w, words in enumerate((w1_words, w2_words)):
-            codes = keep.tile([P, 2, N], I32, name="w_codes%d" % w, align_bytes=64)
-            nc.sync.dma_start(out=codes[:], in_=words.rearrange("z p n t -> p z (n t)").bitcast(I32))
-            w_codes.append(codes)
+        x_rows = xT.rearrange("(z p t) c -> z t p c", p=P, t=4)
+        w1_rows = w1_words.rearrange("z p n t -> p z (n t)").bitcast(I32)
+        w1_codes = [keep.tile([P, N], I32, name="w1_codes%d" % z, align_bytes=64) for z in range(2)]
+        w2_codes = keep.tile([P, 2, N], I32, name="w2_codes", align_bytes=64)
+        w_codes = {(0, 0): w1_codes[0][:], (0, 1): w1_codes[1][:], (1, 0): w2_codes[:, 0, :], (1, 1): w2_codes[:, 1, :]}
+        planes = []
+        for i in range(8):
+            planes.append(keep.tile([P, T], F32, name="plane%d" % i))
+            nc.sync.dma_start(out=planes[i][:], in_=x_rows[i // 4, i % 4])
+            if i == 0:
+                nc.sync.dma_start(offsets[:], offs)
+            if i == 6:
+                nc.sync.dma_start(out=w1_codes[0][:], in_=w1_rows[:, 0, :])
+        nc.sync.dma_start(out=w2_codes[:], in_=w2_words.rearrange("z p n t -> p z (n t)").bitcast(I32))
+        nc.sync.dma_start(out=w1_codes[1][:], in_=w1_rows[:, 1, :])
         res_rows = []
         for b in range(2):
             rows = keep.tile([P, T], F32, name="res%d" % b)
             nc.sync.dma_start(out=rows[:], in_=res[P * b : P * (b + 1), :])
             res_rows.append(rows)
 
-        picked = {}
-        for z in range(2):
-            for half in range(2):
-                picked[z, half] = keep.tile([P, 2, HALF], U32, name="picked%d_%d" % (z, half))
+        for w in range(2):
+            for q in range(4):
+                nc.vector.tensor_copy(w_scale[w][32 * q : 32 * q + 4].bitcast(I32), staged[w][:, :, q, :])
+
+        def gather(on_scalar, dst, window, j0, n):
+            if on_scalar:
+                nc.scalar.activation(dst, window[:].indirect(entries(j0, n)), COPY)
+            else:
+                nc.vector.tensor_copy(dst, window[:].indirect(entries(j0, n)))
+
         x_codes = [keep.tile([P, S], U32, name="x_codes%d" % z, align_bytes=64) for z in range(2)]
         x_scale = [keep.tile([P, S], U8, name="x_scale%d" % z, align_bytes=64) for z in range(2)]
 
-        def round_pair(pair):
-            window = keep.tile([P, 2 * T], BF16, name="window%d" % pair)
-            c0 = 0
-            for load, (width, v_cols) in enumerate(LOADS[pair]):
-                s_cols = width - v_cols
-                src = raw[pair, load][:].rearrange("p t c -> p c t")
-                dst = window[:, 2 * c0 : 2 * (c0 + width)].rearrange("p (c t) -> p c t", t=2)
-                if s_cols:
-                    nc.scalar.copy(dst[:, :s_cols, :], src[:, :s_cols, :])
-                if v_cols:
-                    nc.vector.tensor_copy(dst[:, s_cols:, :], src[:, s_cols:, :])
-                c0 += width
-            return window
-
-        def gather_pair(pair, window, j0, n):
-            z, h = divmod(pair, 2)
-            half, c0 = divmod(j0, HALF)
-            nc.vector.tensor_copy(picked[z, half][:, h, c0 : c0 + n], window[:].bitcast(U32).indirect(entries(j0, n)))
-
-        def weave(z, j0, n):
-            half, c0 = divmod(j0, HALF)
-            woven = keep.tile([P, 4 * n], BF16, name="woven%d_%d" % (z, j0), align_bytes=64)
-            src = picked[z, half][:, :, c0 : c0 + n]
-            if z == 1:
-                nc.scalar.copy(woven[:].bitcast(U32).rearrange("p (n h) -> p n h", h=2), src.rearrange("p h n -> p n h"))
-            else:
-                nc.vector.tensor_copy(
-                    woven[:].bitcast(I32).rearrange("p (n h) -> p n h", h=2), src.bitcast(I32).rearrange("p h n -> p n h")
-                )
-            return woven
+        def place(woven, h, src):
+            nc.vector.tensor_copy(
+                woven[:].rearrange("p (n t) -> p n t", t=4)[:, :, 2 * h : 2 * h + 2], src.rearrange("p t n -> p n t")
+            )
 
         def quantise(z, j0, n, woven):
             nc.vector.quantize_mx(
                 out=x_codes[z][:, j0 : j0 + n].bitcast(FP8X4), scales=x_scale[z][:, j0 : j0 + n], in_=woven[:]
             )
 
-        for pair in range(3):
-            window = round_pair(pair)
-            for j0 in range(0, S, HALF):
-                gather_pair(pair, window, j0, HALF)
-            if pair == 1:
-                woven_halves = [weave(0, j0, HALF) for j0 in range(0, S, HALF)]
-                for half in range(2):
-                    quantise(0, HALF * half, HALF, woven_halves[half])
+        def gather_pair(pair, s_entries):
+            picked = keep.tile([P, 2, S], BF16, name="picked%d" % pair)
+            for t in range(2):
+                gather(True, picked[:, t, :s_entries], planes[2 * pair + t], 0, s_entries)
+                gather(False, picked[:, t, s_entries:], planes[2 * pair + t], s_entries, S - s_entries)
+            return picked
 
-        window = round_pair(3)
-        woven_quarters = []
-        for step in range(S // QUARTER + 1):
-            if step < S // QUARTER:
-                gather_pair(3, window, QUARTER * step, QUARTER)
-                woven_quarters.append(weave(1, QUARTER * step, QUARTER))
-            if step >= 1:
-                quantise(1, QUARTER * (step - 1), QUARTER, woven_quarters[step - 1])
+        woven0 = [keep.tile([P, 4 * HALF], BF16, name="woven0_%d" % half, align_bytes=64) for half in range(2)]
+        for h in range(2):
+            picked = gather_pair(h, HALF)
+            for half in range(2):
+                place(woven0[half], h, picked[:, :, HALF * half : HALF * (half + 1)])
+        for half in range(2):
+            quantise(0, HALF * half, HALF, woven0[half])
+
+        woven1 = [keep.tile([P, 4 * QUARTER], BF16, name="woven1_%d" % q, align_bytes=64) for q in range(4)]
+        picked = gather_pair(2, 3 * QUARTER)
+        for q in range(4):
+            place(woven1[q], 0, picked[:, :, QUARTER * q : QUARTER * (q + 1)])
+        last = {q: keep.tile([P, 2, QUARTER], BF16, name="last%d" % q) for q in range(1, 4)}
+        for t in range(2):
+            gather(False, woven1[0][:].rearrange("p (n t) -> p n t", t=4)[:, :, 2 + t], planes[6 + t], 0, QUARTER)
+            for q in range(1, 4):
+                gather(True, last[q][:, t, :], planes[6 + t], QUARTER * q, QUARTER)
+        for half in range(2):
+            for q in (2 * half, 2 * half + 1):
+                if q in last:
+                    place(woven1[q], 1, last[q][:])
+            for q in (2 * half, 2 * half + 1):
+                quantise(1, QUARTER * q, QUARTER, woven1[q])
 
         def new_bank(number):
             return psum.tile([P, HALF], F32, name="bank%d" % number)
 
-        def product(number, w, b, j0, n):
-            bank = new_bank(number)
-            for z in range(2):
-                nc.tensor.matmul_mx(
-                    out=bank[:, :n],
-                    lhsT=w_codes[w][:, z, P * b : P * (b + 1)].bitcast(FP8X4),
-                    lhsT_scale=scale_plane(w, z, b),
-                    rhs=x_codes[z][:, j0 : j0 + n].bitcast(FP8X4),
-                    rhs_scale=x_scale[z][:, j0 : j0 + n],
-                    start=(z == 0),
-                    stop=(z == 1),
-                )
-            return bank
+        def mx_pass(dst, w, b, j0, z, start, stop):
+            n = dst.shape[1]
+            nc.tensor.matmul_mx(
+                out=dst,
+                lhsT=w_codes[w, z][:, P * b : P * (b + 1)].bitcast(FP8X4),
+                lhsT_scale=w_scale[w][:, z, P * b : P * (b + 1)],
+                rhs=x_codes[z][:, j0 : j0 + n].bitcast(FP8X4),
+                rhs_scale=x_scale[z][:, j0 : j0 + n],
+                start=start,
+                stop=stop,
+            )
 
-        def turned_gate_product(number, half):
-            bank = new_bank(number)
-            for i in range(HALF // P):
-                j0 = HALF * half + P * i
-                for z in range(2):
-                    nc.tensor.matmul_mx(
-                        out=bank[:, P * i : P * (i + 1)],
-                        lhsT=x_codes[z][:, j0 : j0 + P].bitcast(FP8X4),
-                        lhsT_scale=x_scale[z][:, j0 : j0 + P],
-                        rhs=w_codes[1][:, z, 0:P].bitcast(FP8X4),
-                        rhs_scale=scale_plane(1, z, 0),
-                        start=(z == 0),
-                        stop=(z == 1),
-                    )
-            return bank
-
-        def turn(bank, src, start, stop):
-            last = HALF // P - 1
-            for i in range(HALF // P):
-                cols = slice(P * i, P * (i + 1))
-                nc.tensor.matmul(
-                    bank[:, cols], src[:, cols], ident[:], start=start and i == 0, stop=stop and i == last, is_transpose=True
-                )
 
         def new_tile(name, half):
             return keep.tile([P, HALF], F32, name="%s%d" % (name, half))
@@ -198,97 +150,87 @@ def tile_picked_highway_tanh_l_kernel(
         def tanh(dst, src, scale):
             nc.scalar.activation(dst, src, TANH, bias=zero[:], scale=scale)
 
-        u_y0_quarters = [product(quarter, 0, 0, QUARTER * quarter, QUARTER) for quarter in range(2)]
-        u_y1_first = product(2, 0, 1, 0, HALF)
-        u_gate0_first = turned_gate_product(3, 0)
-        u_gate0_second = turned_gate_product(5, 1)
-        u_y0_second = product(6, 0, 0, HALF, HALF)
-        u_gate1_first = product(4, 1, 1, 0, HALF)
-        u_y1_second = product(7, 0, 1, HALF, HALF)
+        first = [new_bank(0), new_bank(1)]
+        later = [(1, 0), (0, 1), (1, 1)]
+        u_y = {part: new_bank(2 + 2 * i) for i, part in enumerate(later)}
+        u_g = {part: new_bank(3 + 2 * i) for i, part in enumerate(later)}
+        for q in range(2):
+            mx_pass(first[q][:, :QUARTER], 0, 0, QUARTER * q, 0, True, False)
+        for b, half in later:
+            mx_pass(u_y[b, half][:], 0, b, HALF * half, 0, True, False)
+        for q in range(2):
+            mx_pass(first[q][:, QUARTER:], 1, 0, QUARTER * q, 0, False, False)
+        mx_pass(u_g[1, 0][:], 1, 1, 0, 0, True, False)
+        for q in range(2):
+            mx_pass(first[q][:, :QUARTER], 0, 0, QUARTER * q, 1, False, False)
+            mx_pass(first[q][:, QUARTER:], 1, 0, QUARTER * q, 1, False, True)
+        for b, half in later:
+            mx_pass(u_y[b, half][:], 0, b, HALF * half, 1, False, True)
+            if half == 1:
+                mx_pass(u_g[b, half][:], 1, b, HALF * half, 0, True, False)
+            mx_pass(u_g[b, half][:], 1, b, HALF * half, 1, False, True)
 
-        r0 = []
-        for half in range(2):
-            r0.append(new_tile("r0_", half))
-            nc.vector.tensor_copy(r0[half][:], res_rows[0][:].indirect(entries(HALF * half, HALF)))
+        y = {(b, half): new_tile("y%d_" % b, half) for b in range(2) for half in range(2)}
+        s = {(b, half): new_tile("s%d_" % b, half) for b in range(2) for half in range(2)}
+        for q in range(2):
+            cols = slice(QUARTER * q, QUARTER * (q + 1))
+            tanh(y[0, 0][:, cols], first[q][:, :QUARTER], 1.0)
+            tanh(s[0, 0][:, cols], first[q][:, QUARTER:], 0.5)
+        for part in later:
+            tanh(y[part][:], u_y[part][:], 1.0)
+            tanh(s[part][:], u_g[part][:], 0.5)
 
-        minus_y0, s0, y1, s1 = {}, {}, {}, {}
-        minus_y0[0] = new_tile("minus_y0_", 0)
-        for quarter, bank in enumerate(u_y0_quarters):
-            tanh(minus_y0[0][:, QUARTER * quarter : QUARTER * (quarter + 1)], bank[:, :QUARTER], -1.0)
-        y1[0] = new_tile("y1_", 0)
-        tanh(y1[0][:], u_y1_first[:], 1.0)
-        for half, bank in enumerate((u_gate0_first, u_gate0_second)):
-            s0[half] = new_tile("s0_", half)
-            tanh(s0[half][:], bank[:], 0.5)
-        minus_y0[1] = new_tile("minus_y0_", 1)
-        tanh(minus_y0[1][:], u_y0_second[:], -1.0)
-        s1[0] = new_tile("s1_", 0)
-        tanh(s1[0][:], u_gate1_first[:], 0.5)
-        y1[1] = new_tile("y1_", 1)
-        tanh(y1[1][:], u_y1_second[:], 1.0)
-
-        d0 = []
-        for half, number in enumerate((5, 3)):
-            d0.append(new_bank(number))
-            turn(d0[half], minus_y0[half], True, False)
-            turn(d0[half], r0[half], False, True)
-        minus_2r0 = []
-        for half, number in enumerate((2, 6)):
-            bank = new_bank(number)
-            turn(bank, r0[half], True, True)
-            minus_2r0.append(new_tile("minus_2r0_", half))
-            nc.scalar.activation(minus_2r0[half][:], bank[:], COPY, scale=-2.0)
-
-        u_gate1_second = product(7, 1, 1, HALF, HALF)
-
-        e0, sum0, d1 = {}, {}, {}
-
-        def open_sum0(half):
-            sum0[half] = new_bank(half)
-            turn(sum0[half], minus_2r0[half], True, False)
-
-        def multiply0(half):
-            e0[half] = new_tile("e0_", half)
-            nc.vector.scalar_tensor_tensor(e0[half][:], s0[half][:], 1.0, d0[half][:], ALU.add, ALU.mult)
-
-        def finish0(half):
-            turn(sum0[half], e0[half], False, True)
-            out0 = new_tile("out0_", half)
-            nc.scalar.activation(out0[:], sum0[half][:], COPY, scale=-0.5)
-            nc.scalar.dma_start(out=out[0:P, HALF * half : HALF * (half + 1)], in_=out0[:])
-
-        def stretch(tiles, nr):
-            j0, n = STRETCHES[nr]
+        def piece_of(tiles, piece):
+            b, j0, n = piece
             half, c0 = divmod(j0, HALF)
-            return tiles[half][:, c0 : c0 + n]
+            return tiles[b, half][:, c0 : c0 + n]
 
-        def subtract1(nr, dst):
-            j0, n = STRETCHES[nr]
-            d1[nr] = dst
-            nc.vector.tensor_tensor(dst, res_rows[1][:].indirect(entries(j0, n)), stretch(y1, nr), ALU.subtract)
+        def store(piece, src):
+            b, j0, n = piece
+            nc.sync.dma_start(out=out[P * b : P * (b + 1), j0 : j0 + n], in_=src)
 
-        def multiply1(nr):
-            nc.vector.scalar_tensor_tensor(stretch(s1, nr), stretch(s1, nr), 1.0, d1[nr], ALU.subtract, ALU.mult)
+        fused = [(0, 0, HALF), (1, HALF + QUARTER, QUARTER)]
+        split = [(0, HALF, HALF), (1, 0, HALF), (1, HALF, QUARTER)]
+        picked_r = {}
+        for b, j0, n in fused + split:
+            picked_r[b, j0, n] = keep.tile([P, n], F32, name="picked_r%d_%d" % (b, j0))
+        for b, j0, n in split:
+            nc.scalar.activation(picked_r[b, j0, n][:], res_rows[b][:].indirect(entries(j0, n)), COPY, scale=0.5)
 
-        def finish1(nr):
-            j0, n = STRETCHES[nr]
-            nc.vector.scalar_tensor_tensor(d1[nr], stretch(s1, nr), -0.5, stretch(y1, nr), ALU.mult, ALU.add)
-            nc.sync.dma_start(out=out[P : 2 * P, j0 : j0 + n], in_=d1[nr])
+        def difference(piece):
+            b, j0, n = piece
+            nc.vector.tensor_tensor(picked_r[piece][:], res_rows[b][:].indirect(entries(j0, n)), piece_of(y, piece), ALU.subtract)
 
-        d1_first = new_tile("d1_", 0)
-        subtract1(0, d1_first[:])
-        open_sum0(0)
-        multiply0(0)
-        multiply1(0)
-        open_sum0(1)
-        multiply0(1)
-        finish1(0)
-        s1[1] = new_tile("s1_", 1)
-        tanh(s1[1][:], u_gate1_second[:], 0.5)
+        def gated_r(piece):
+            nc.vector.scalar_tensor_tensor(piece_of(s, piece), piece_of(s, piece), 1.0, picked_r[piece][:], ALU.subtract, ALU.mult)
 
-        for nr in (1, 2):
-            finish0(nr - 1)
-            subtract1(nr, stretch(s0, nr))
-        for stage in (multiply1, finish1):
-            for nr in (1, 2):
-                stage(nr)
+        def finish_fused(piece):
+            nc.vector.scalar_tensor_tensor(picked_r[piece][:], piece_of(s, piece), -0.5, piece_of(y, piece), ALU.mult, ALU.add)
+            store(piece, picked_r[piece][:])
+
+        def gated_y(piece):
+            nc.vector.scalar_tensor_tensor(piece_of(y, piece), piece_of(s, piece), 1.0, piece_of(y, piece), ALU.add, ALU.mult)
+
+        def finish_split(piece, c0, n):
+            b, j0 = piece[:2]
+            part = (b, j0 + c0, n)
+            dst = picked_r[piece][:, c0 : c0 + n]
+            nc.vector.scalar_tensor_tensor(dst, piece_of(y, part), 0.5, piece_of(s, part), ALU.mult, ALU.subtract)
+            store(part, dst)
+
+        difference(fused[0])
+        gated_y(split[1])
+        gated_r(fused[0])
+        gated_y(split[0])
+        finish_fused(fused[0])
+        gated_y(split[2])
+        difference(fused[1])
+        gated_r(split[0])
+        gated_r(fused[1])
+        finish_split(split[0], 0, HALF)
+        gated_r(split[1])
+        finish_fused(fused[1])
+        finish_split(split[1], 0, QUARTER)
+        gated_r(split[2])
+        finish_split(split[1], QUARTER, QUARTER)
+        finish_split(split[2], 0, QUARTER)

@@ -1,6 +1,7 @@
 from contextlib import ExitStack
 
 import concourse.mybir as mybir
+from concourse.masks import make_identity
 
 K, T, S, N = 1024, 2048, 1024, 256
 FLOPS = 2 * 2 * K * N * S
@@ -14,6 +15,7 @@ U8 = mybir.dt.uint8
 FP8X4 = mybir.dt.float8_e4m3fn_x4
 ALU = mybir.AluOpType
 TANH = mybir.ActivationFunctionType.Tanh
+SIGMOID = mybir.ActivationFunctionType.Sigmoid
 COPY = mybir.ActivationFunctionType.Copy
 
 P = 128
@@ -45,8 +47,11 @@ def tile_picked_highway_tanh_l_kernel(
 
         zero_in = keep.tile([P, 1], F32, name="zero_in")
         zero = keep.tile([P, 1], F32, name="zero")
-        nc.vector.memset(zero_in[:], 0.0)
-        nc.scalar.activation(zero[:], zero_in[:], TANH)
+        nc.vector.memset(zero_in[:], -200.0)
+        nc.scalar.activation(zero[:], zero_in[:], SIGMOID)
+
+        ident = keep.tile([P, P], F32, name="ident")
+        make_identity(nc, ident[:])
 
         w_scale = []
         for w in range(2):
@@ -147,90 +152,117 @@ def tile_picked_highway_tanh_l_kernel(
         def new_tile(name, half):
             return keep.tile([P, HALF], F32, name="%s%d" % (name, half))
 
-        def tanh(dst, src, scale):
-            nc.scalar.activation(dst, src, TANH, bias=zero[:], scale=scale)
 
-        first = [new_bank(0), new_bank(1)]
-        later = [(1, 0), (0, 1), (1, 1)]
-        u_y = {part: new_bank(2 + 2 * i) for i, part in enumerate(later)}
-        u_g = {part: new_bank(3 + 2 * i) for i, part in enumerate(later)}
-        for q in range(2):
-            mx_pass(first[q][:, :QUARTER], 0, 0, QUARTER * q, 0, True, False)
-        for b, half in later:
-            mx_pass(u_y[b, half][:], 0, b, HALF * half, 0, True, False)
-        for q in range(2):
-            mx_pass(first[q][:, QUARTER:], 1, 0, QUARTER * q, 0, False, False)
-        mx_pass(u_g[1, 0][:], 1, 1, 0, 0, True, False)
-        for q in range(2):
-            mx_pass(first[q][:, :QUARTER], 0, 0, QUARTER * q, 1, False, False)
-            mx_pass(first[q][:, QUARTER:], 1, 0, QUARTER * q, 1, False, True)
-        for b, half in later:
-            mx_pass(u_y[b, half][:], 0, b, HALF * half, 1, False, True)
-            if half == 1:
-                mx_pass(u_g[b, half][:], 1, b, HALF * half, 0, True, False)
-            mx_pass(u_g[b, half][:], 1, b, HALF * half, 1, False, True)
+        def turned_gate_pass(bank, part, z):
+            b, half = part
+            for i in range(HALF // P):
+                j0 = HALF * half + P * i
+                nc.tensor.matmul_mx(
+                    out=bank[:, P * i : P * (i + 1)],
+                    lhsT=x_codes[z][:, j0 : j0 + P].bitcast(FP8X4),
+                    lhsT_scale=x_scale[z][:, j0 : j0 + P],
+                    rhs=w_codes[1, z][:, P * b : P * (b + 1)].bitcast(FP8X4),
+                    rhs_scale=w_scale[1][:, z, P * b : P * (b + 1)],
+                    start=(z == 0 and i == 0),
+                    stop=(z == 1 and i == HALF // P - 1),
+                )
 
-        y = {(b, half): new_tile("y%d_" % b, half) for b in range(2) for half in range(2)}
-        s = {(b, half): new_tile("s%d_" % b, half) for b in range(2) for half in range(2)}
+        def turn(bank, src, start, stop):
+            squares = src.shape[1] // P
+            for i in range(squares):
+                cols = slice(P * i, P * (i + 1))
+                nc.tensor.matmul(
+                    bank[:, cols], src[:, cols], ident[:], start=start and i == 0, stop=stop and i == squares - 1, is_transpose=True
+                )
+
+        parts = [(0, 0), (0, 1), (1, 0), (1, 1)]
+        u_first = [new_bank(0), new_bank(7)]
+        u_y = {part: new_bank(i) for i, part in enumerate(parts) if i > 0}
+        u_g = {part: new_bank(4 + i) for i, part in enumerate(parts[:3])}
+
+        def y_pass(part, z):
+            mx_pass(u_y[part][:], 0, part[0], HALF * part[1], z, z == 0, z == 1)
+
+        def first_pass(q, z):
+            mx_pass(u_first[q][:, :QUARTER], 0, 0, QUARTER * q, z, z == 0, z == 1)
+
+        y = {part: new_tile("y%d_" % part[0], part[1]) for part in parts}
+        gate = {}
+
+        def make_y(part):
+            nc.scalar.activation(y[part][:], u_y[part][:], TANH, bias=zero[:])
+
+        def make_gate(part, number):
+            turned = new_tile("gate%d_" % part[0], part[1])
+            nc.scalar.activation(turned[:], u_g[part][:], SIGMOID, bias=zero[:])
+            gate[part] = new_bank(number)
+            turn(gate[part], turned[:], True, True)
+
         for q in range(2):
-            cols = slice(QUARTER * q, QUARTER * (q + 1))
-            tanh(y[0, 0][:, cols], first[q][:, :QUARTER], 1.0)
-            tanh(s[0, 0][:, cols], first[q][:, QUARTER:], 0.5)
-        for part in later:
-            tanh(y[part][:], u_y[part][:], 1.0)
-            tanh(s[part][:], u_g[part][:], 0.5)
+            first_pass(q, 0)
+        for part in parts[1:]:
+            y_pass(part, 0)
+        turned_gate_pass(u_g[0, 0], (0, 0), 0)
+        for q in range(2):
+            first_pass(q, 1)
+            nc.scalar.activation(y[0, 0][:, QUARTER * q : QUARTER * (q + 1)], u_first[q][:, :QUARTER], TANH, bias=zero[:])
+        y_pass((1, 0), 1)
+        turned_gate_pass(u_g[0, 0], (0, 0), 1)
+        make_y((1, 0))
+        turned_gate_pass(u_g[0, 1], (0, 1), 0)
+        y_pass((0, 1), 1)
+        turned_gate_pass(u_g[0, 1], (0, 1), 1)
+        make_gate((0, 0), 0)
+        make_y((0, 1))
+        for z in range(2):
+            turned_gate_pass(u_g[1, 0], (1, 0), z)
+        make_gate((0, 1), 2)
+        u_g[1, 1] = new_bank(7)
+        for z in range(2):
+            turned_gate_pass(u_g[1, 1], (1, 1), z)
+        make_gate((1, 0), 4)
+        y_pass((1, 1), 1)
+        make_gate((1, 1), 1)
+        make_y((1, 1))
 
         def piece_of(tiles, piece):
             b, j0, n = piece
             half, c0 = divmod(j0, HALF)
             return tiles[b, half][:, c0 : c0 + n]
 
-        def store(piece, src):
-            b, j0, n = piece
-            nc.sync.dma_start(out=out[P * b : P * (b + 1), j0 : j0 + n], in_=src)
-
-        fused = [(0, 0, HALF), (1, HALF + QUARTER, QUARTER)]
-        split = [(0, HALF, HALF), (1, 0, HALF), (1, HALF, QUARTER)]
+        fused = [(0, 0, HALF), (0, HALF, HALF)]
+        split = [(1, 0, HALF), (1, HALF, QUARTER), (1, HALF + QUARTER, QUARTER)]
         picked_r = {}
         for b, j0, n in fused + split:
             picked_r[b, j0, n] = keep.tile([P, n], F32, name="picked_r%d_%d" % (b, j0))
         for b, j0, n in split:
-            nc.scalar.activation(picked_r[b, j0, n][:], res_rows[b][:].indirect(entries(j0, n)), COPY, scale=0.5)
+            nc.scalar.activation(picked_r[b, j0, n][:], res_rows[b][:].indirect(entries(j0, n)), COPY)
 
         def difference(piece):
             b, j0, n = piece
             nc.vector.tensor_tensor(picked_r[piece][:], res_rows[b][:].indirect(entries(j0, n)), piece_of(y, piece), ALU.subtract)
 
         def gated_r(piece):
-            nc.vector.scalar_tensor_tensor(piece_of(s, piece), piece_of(s, piece), 1.0, picked_r[piece][:], ALU.subtract, ALU.mult)
-
-        def finish_fused(piece):
-            nc.vector.scalar_tensor_tensor(picked_r[piece][:], piece_of(s, piece), -0.5, piece_of(y, piece), ALU.mult, ALU.add)
-            store(piece, picked_r[piece][:])
+            nc.vector.scalar_tensor_tensor(picked_r[piece][:], piece_of(gate, piece), 1.0, picked_r[piece][:], ALU.subtract, ALU.mult)
 
         def gated_y(piece):
-            nc.vector.scalar_tensor_tensor(piece_of(y, piece), piece_of(s, piece), 1.0, piece_of(y, piece), ALU.add, ALU.mult)
+            nc.vector.tensor_tensor(piece_of(y, piece), piece_of(gate, piece), piece_of(y, piece), ALU.mult)
 
-        def finish_split(piece, c0, n):
-            b, j0 = piece[:2]
-            part = (b, j0 + c0, n)
-            dst = picked_r[piece][:, c0 : c0 + n]
-            nc.vector.scalar_tensor_tensor(dst, piece_of(y, part), 0.5, piece_of(s, part), ALU.mult, ALU.subtract)
-            store(part, dst)
+        def finish(engine, piece):
+            b, j0, n = piece
+            engine.tensor_tensor(picked_r[piece][:], piece_of(y, piece), picked_r[piece][:], ALU.subtract)
+            nc.sync.dma_start(out=out[P * b : P * (b + 1), j0 : j0 + n], in_=picked_r[piece][:])
 
-        difference(fused[0])
-        gated_y(split[1])
-        gated_r(fused[0])
-        gated_y(split[0])
-        finish_fused(fused[0])
-        gated_y(split[2])
-        difference(fused[1])
+        for piece in fused:
+            difference(piece)
+        for piece in fused:
+            gated_r(piece)
+            finish(nc.gpsimd, piece)
+        for half in range(2):
+            gated_y((1, HALF * half, HALF))
         gated_r(split[0])
-        gated_r(fused[1])
-        finish_split(split[0], 0, HALF)
         gated_r(split[1])
-        finish_fused(fused[1])
-        finish_split(split[1], 0, QUARTER)
+        finish(nc.vector, split[0])
         gated_r(split[2])
-        finish_split(split[1], QUARTER, QUARTER)
-        finish_split(split[2], 0, QUARTER)
+        finish(nc.vector, split[1])
+        finish(nc.vector, split[2])

@@ -176,54 +176,52 @@ def tile_picked_highway_tanh_l_kernel(
                 )
 
         parts = [(0, 0), (0, 1), (1, 0), (1, 1)]
-        u_first = [new_bank(0), new_bank(7)]
-        u_y = {part: new_bank(i) for i, part in enumerate(parts) if i > 0}
-        u_g = {part: new_bank(4 + i) for i, part in enumerate(parts[:3])}
+        first = [new_bank(0), new_bank(1)]
+        u_y = {part: new_bank(1 + i) for i, part in enumerate(parts) if i > 0}
+        u_g = {part: new_bank(4 + i) for i, part in enumerate(parts) if i > 0}
 
         def y_pass(part, z):
             mx_pass(u_y[part][:], 0, part[0], HALF * part[1], z, z == 0, z == 1)
 
-        def first_pass(q, z):
-            mx_pass(u_first[q][:, :QUARTER], 0, 0, QUARTER * q, z, z == 0, z == 1)
-
-        y = {part: new_tile("y%d_" % part[0], part[1]) for part in parts}
-        gate = {}
-
-        def make_y(part):
-            nc.scalar.activation(y[part][:], u_y[part][:], TANH, bias=zero[:])
-
-        def make_gate(part, number):
-            turned = new_tile("gate%d_" % part[0], part[1])
-            nc.scalar.activation(turned[:], u_g[part][:], SIGMOID, bias=zero[:])
-            gate[part] = new_bank(number)
-            turn(gate[part], turned[:], True, True)
-
         for q in range(2):
-            first_pass(q, 0)
+            mx_pass(first[q][:, :QUARTER], 0, 0, QUARTER * q, 0, True, False)
         for part in parts[1:]:
             y_pass(part, 0)
-        turned_gate_pass(u_g[0, 0], (0, 0), 0)
         for q in range(2):
-            first_pass(q, 1)
-            nc.scalar.activation(y[0, 0][:, QUARTER * q : QUARTER * (q + 1)], u_first[q][:, :QUARTER], TANH, bias=zero[:])
-        y_pass((1, 0), 1)
-        turned_gate_pass(u_g[0, 0], (0, 0), 1)
-        make_y((1, 0))
-        turned_gate_pass(u_g[0, 1], (0, 1), 0)
+            mx_pass(first[q][:, QUARTER:], 1, 0, QUARTER * q, 0, False, False)
+        turned_gate_pass(u_g[1, 0], (1, 0), 0)
+        for q in range(2):
+            mx_pass(first[q][:, :QUARTER], 0, 0, QUARTER * q, 1, False, False)
+            mx_pass(first[q][:, QUARTER:], 1, 0, QUARTER * q, 1, False, True)
+        turned_gate_pass(u_g[1, 0], (1, 0), 1)
+        mx_pass(u_g[0, 1][:], 1, 0, HALF, 0, True, False)
+        turned_gate_pass(u_g[1, 1], (1, 1), 0)
         y_pass((0, 1), 1)
-        turned_gate_pass(u_g[0, 1], (0, 1), 1)
-        make_gate((0, 0), 0)
-        make_y((0, 1))
-        for z in range(2):
-            turned_gate_pass(u_g[1, 0], (1, 0), z)
-        make_gate((0, 1), 2)
-        u_g[1, 1] = new_bank(7)
-        for z in range(2):
-            turned_gate_pass(u_g[1, 1], (1, 1), z)
-        make_gate((1, 0), 4)
-        y_pass((1, 1), 1)
-        make_gate((1, 1), 1)
-        make_y((1, 1))
+        turned_gate_pass(u_g[1, 1], (1, 1), 1)
+        mx_pass(u_g[0, 1][:], 1, 0, HALF, 1, False, True)
+        for half in range(2):
+            y_pass((1, half), 1)
+
+        y = {part: new_tile("y%d_" % part[0], part[1]) for part in parts}
+        gate = {part: new_tile("gate%d_" % part[0], part[1]) for part in parts}
+
+        def activate(dst, src, func):
+            nc.scalar.activation(dst, src, func, bias=zero[:])
+
+        for q in range(2):
+            cols = slice(QUARTER * q, QUARTER * (q + 1))
+            activate(y[0, 0][:, cols], first[q][:, :QUARTER], TANH)
+            activate(gate[0, 0][:, cols], first[q][:, QUARTER:], SIGMOID)
+        activate(gate[1, 0][:], u_g[1, 0][:], SIGMOID)
+        activate(y[0, 1][:], u_y[0, 1][:], TANH)
+        activate(gate[1, 1][:], u_g[1, 1][:], SIGMOID)
+        activate(gate[0, 1][:], u_g[0, 1][:], SIGMOID)
+        for half in range(2):
+            activate(y[1, half][:], u_y[1, half][:], TANH)
+        for half in range(2):
+            turned = gate[1, half]
+            gate[1, half] = new_bank(half)
+            turn(gate[1, half], turned[:], True, True)
 
         def piece_of(tiles, piece):
             b, j0, n = piece
@@ -248,21 +246,24 @@ def tile_picked_highway_tanh_l_kernel(
         def gated_y(piece):
             nc.vector.tensor_tensor(piece_of(y, piece), piece_of(gate, piece), piece_of(y, piece), ALU.mult)
 
-        def finish(engine, piece):
-            b, j0, n = piece
-            engine.tensor_tensor(picked_r[piece][:], piece_of(y, piece), picked_r[piece][:], ALU.subtract)
-            nc.sync.dma_start(out=out[P * b : P * (b + 1), j0 : j0 + n], in_=picked_r[piece][:])
+        def finish(engine, piece, c0, n):
+            b, j0 = piece[:2]
+            dst = picked_r[piece][:, c0 : c0 + n]
+            engine.tensor_tensor(dst, piece_of(y, (b, j0 + c0, n)), dst, ALU.subtract)
+            nc.sync.dma_start(out=out[P * b : P * (b + 1), j0 + c0 : j0 + c0 + n], in_=dst)
 
-        for piece in fused:
-            difference(piece)
-        for piece in fused:
-            gated_r(piece)
-            finish(nc.gpsimd, piece)
+        for stage in (difference, gated_r):
+            for piece in fused:
+                stage(piece)
+        finish(nc.gpsimd, fused[0], 0, HALF)
+        finish(nc.gpsimd, fused[1], 0, QUARTER)
         for half in range(2):
             gated_y((1, HALF * half, HALF))
         gated_r(split[0])
         gated_r(split[1])
-        finish(nc.vector, split[0])
+        finish(nc.vector, split[0], 0, QUARTER)
         gated_r(split[2])
-        finish(nc.vector, split[1])
-        finish(nc.vector, split[2])
+        finish(nc.vector, split[0], QUARTER, QUARTER)
+        finish(nc.vector, fused[1], QUARTER, QUARTER)
+        finish(nc.vector, split[1], 0, QUARTER)
+        finish(nc.vector, split[2], 0, QUARTER)

@@ -21,6 +21,7 @@ COPY = mybir.ActivationFunctionType.Copy
 P = 128
 HALF = 512
 QUARTER = 256
+EIGHTH = 128
 
 
 def tile_picked_highway_tanh_l_kernel(
@@ -194,11 +195,11 @@ def tile_picked_highway_tanh_l_kernel(
             mx_pass(first[q][:, :QUARTER], 0, 0, QUARTER * q, 1, False, False)
             mx_pass(first[q][:, QUARTER:], 1, 0, QUARTER * q, 1, False, True)
         turned_gate_pass(u_g[1, 0], (1, 0), 1)
-        mx_pass(u_g[0, 1][:], 1, 0, HALF, 0, True, False)
-        turned_gate_pass(u_g[1, 1], (1, 1), 0)
+        for b in range(2):
+            turned_gate_pass(u_g[b, 1], (b, 1), 0)
         y_pass((0, 1), 1)
-        turned_gate_pass(u_g[1, 1], (1, 1), 1)
-        mx_pass(u_g[0, 1][:], 1, 0, HALF, 1, False, True)
+        for b in range(2):
+            turned_gate_pass(u_g[b, 1], (b, 1), 1)
         for half in range(2):
             y_pass((1, half), 1)
 
@@ -214,14 +215,14 @@ def tile_picked_highway_tanh_l_kernel(
             activate(gate[0, 0][:, cols], first[q][:, QUARTER:], SIGMOID)
         activate(gate[1, 0][:], u_g[1, 0][:], SIGMOID)
         activate(y[0, 1][:], u_y[0, 1][:], TANH)
-        activate(gate[1, 1][:], u_g[1, 1][:], SIGMOID)
         activate(gate[0, 1][:], u_g[0, 1][:], SIGMOID)
+        activate(gate[1, 1][:], u_g[1, 1][:], SIGMOID)
         for half in range(2):
             activate(y[1, half][:], u_y[1, half][:], TANH)
-        for half in range(2):
-            turned = gate[1, half]
-            gate[1, half] = new_bank(half)
-            turn(gate[1, half], turned[:], True, True)
+        turned = {part: gate[part] for part in parts[1:]}
+        for number, part in enumerate(parts[1:]):
+            gate[part] = new_bank(number)
+            turn(gate[part], turned[part][:], True, True)
 
         def piece_of(tiles, piece):
             b, j0, n = piece
@@ -240,30 +241,35 @@ def tile_picked_highway_tanh_l_kernel(
             b, j0, n = piece
             nc.vector.tensor_tensor(picked_r[piece][:], res_rows[b][:].indirect(entries(j0, n)), piece_of(y, piece), ALU.subtract)
 
+        gated = {piece: picked_r[piece] for piece in fused + split}
+        gated[split[0]] = turned[1, 0]
+
         def gated_r(piece):
-            nc.vector.scalar_tensor_tensor(picked_r[piece][:], piece_of(gate, piece), 1.0, picked_r[piece][:], ALU.subtract, ALU.mult)
+            nc.vector.scalar_tensor_tensor(gated[piece][:], piece_of(gate, piece), 1.0, picked_r[piece][:], ALU.subtract, ALU.mult)
 
         def gated_y(piece):
             nc.vector.tensor_tensor(piece_of(y, piece), piece_of(gate, piece), piece_of(y, piece), ALU.mult)
 
-        def finish(engine, piece, c0, n):
+        def finish(engine, piece, c0, n, dst):
             b, j0 = piece[:2]
-            dst = picked_r[piece][:, c0 : c0 + n]
-            engine.tensor_tensor(dst, piece_of(y, (b, j0 + c0, n)), dst, ALU.subtract)
+            engine.tensor_tensor(dst, piece_of(y, (b, j0 + c0, n)), gated[piece][:, c0 : c0 + n], ALU.subtract)
             nc.sync.dma_start(out=out[P * b : P * (b + 1), j0 + c0 : j0 + c0 + n], in_=dst)
+
+        def finish_in_place(engine, piece, c0, n):
+            finish(engine, piece, c0, n, gated[piece][:, c0 : c0 + n])
 
         for stage in (difference, gated_r):
             for piece in fused:
                 stage(piece)
-        finish(nc.gpsimd, fused[0], 0, HALF)
-        finish(nc.gpsimd, fused[1], 0, QUARTER)
+        finish_in_place(nc.gpsimd, fused[0], 0, HALF)
+        finish_in_place(nc.gpsimd, fused[1], 0, HALF - EIGHTH)
         for half in range(2):
             gated_y((1, HALF * half, HALF))
         gated_r(split[0])
         gated_r(split[1])
-        finish(nc.vector, split[0], 0, QUARTER)
+        finish_in_place(nc.vector, split[0], 0, QUARTER)
         gated_r(split[2])
-        finish(nc.vector, split[0], QUARTER, QUARTER)
-        finish(nc.vector, fused[1], QUARTER, QUARTER)
-        finish(nc.vector, split[1], 0, QUARTER)
-        finish(nc.vector, split[2], 0, QUARTER)
+        finish(nc.vector, fused[1], HALF - EIGHTH, EIGHTH, picked_r[split[0]][:, :EIGHTH])
+        finish_in_place(nc.vector, split[0], QUARTER, QUARTER)
+        finish_in_place(nc.vector, split[1], 0, QUARTER)
+        finish_in_place(nc.vector, split[2], 0, QUARTER)

@@ -21,7 +21,8 @@ COPY = mybir.ActivationFunctionType.Copy
 P = 128
 HALF = 512
 QUARTER = 256
-EIGHTH = 128
+
+LEFT_TO_VECTOR = 128
 
 
 def tile_picked_highway_tanh_l_kernel(
@@ -46,10 +47,10 @@ def tile_picked_highway_tanh_l_kernel(
             )
             staged.append(rows)
 
-        zero_in = keep.tile([P, 1], F32, name="zero_in")
+        far_left = keep.tile([P, 1], F32, name="far_left")
         zero = keep.tile([P, 1], F32, name="zero")
-        nc.vector.memset(zero_in[:], -200.0)
-        nc.scalar.activation(zero[:], zero_in[:], SIGMOID)
+        nc.vector.memset(far_left[:], -200.0)
+        nc.scalar.activation(zero[:], far_left[:], SIGMOID)
 
         ident = keep.tile([P, P], F32, name="ident")
         make_identity(nc, ident[:])
@@ -65,13 +66,17 @@ def tile_picked_highway_tanh_l_kernel(
         w2_codes = keep.tile([P, 2, N], I32, name="w2_codes", align_bytes=64)
         w_codes = {(0, 0): w1_codes[0][:], (0, 1): w1_codes[1][:], (1, 0): w2_codes[:, 0, :], (1, 1): w2_codes[:, 1, :]}
         planes = []
-        for i in range(8):
+
+        def load_plane(i):
             planes.append(keep.tile([P, T], F32, name="plane%d" % i))
             nc.sync.dma_start(out=planes[i][:], in_=x_rows[i // 4, i % 4])
-            if i == 0:
-                nc.sync.dma_start(offsets[:], offs)
-            if i == 6:
-                nc.sync.dma_start(out=w1_codes[0][:], in_=w1_rows[:, 0, :])
+
+        load_plane(0)
+        nc.sync.dma_start(offsets[:], offs)
+        for i in range(1, 7):
+            load_plane(i)
+        nc.sync.dma_start(out=w1_codes[0][:], in_=w1_rows[:, 0, :])
+        load_plane(7)
         nc.sync.dma_start(out=w2_codes[:], in_=w2_words.rearrange("z p n t -> p z (n t)").bitcast(I32))
         nc.sync.dma_start(out=w1_codes[1][:], in_=w1_rows[:, 1, :])
         res_rows = []
@@ -84,54 +89,56 @@ def tile_picked_highway_tanh_l_kernel(
             for q in range(4):
                 nc.vector.tensor_copy(w_scale[w][32 * q : 32 * q + 4].bitcast(I32), staged[w][:, :, q, :])
 
-        def gather(on_scalar, dst, window, j0, n):
-            if on_scalar:
-                nc.scalar.activation(dst, window[:].indirect(entries(j0, n)), COPY)
-            else:
-                nc.vector.tensor_copy(dst, window[:].indirect(entries(j0, n)))
+        def scalar_gather(dst, window, j0, n):
+            nc.scalar.activation(dst, window[:].indirect(entries(j0, n)), COPY)
+
+        def vector_gather(dst, window, j0, n):
+            nc.vector.tensor_copy(dst, window[:].indirect(entries(j0, n)))
 
         x_codes = [keep.tile([P, S], U32, name="x_codes%d" % z, align_bytes=64) for z in range(2)]
         x_scale = [keep.tile([P, S], U8, name="x_scale%d" % z, align_bytes=64) for z in range(2)]
 
-        def place(woven, h, src):
-            nc.vector.tensor_copy(
-                woven[:].rearrange("p (n t) -> p n t", t=4)[:, :, 2 * h : 2 * h + 2], src.rearrange("p t n -> p n t")
-            )
+        def places(woven):
+            return woven[:].rearrange("p (n t) -> p n t", t=4)
+
+        def weave(woven, h, two_planes):
+            nc.vector.tensor_copy(places(woven)[:, :, 2 * h : 2 * h + 2], two_planes.rearrange("p u n -> p n u"))
 
         def quantise(z, j0, n, woven):
             nc.vector.quantize_mx(
                 out=x_codes[z][:, j0 : j0 + n].bitcast(FP8X4), scales=x_scale[z][:, j0 : j0 + n], in_=woven[:]
             )
 
-        def gather_pair(pair, s_entries):
-            picked = keep.tile([P, 2, S], BF16, name="picked%d" % pair)
-            for t in range(2):
-                gather(True, picked[:, t, :s_entries], planes[2 * pair + t], 0, s_entries)
-                gather(False, picked[:, t, s_entries:], planes[2 * pair + t], s_entries, S - s_entries)
-            return picked
-
         woven0 = [keep.tile([P, 4 * HALF], BF16, name="woven0_%d" % half, align_bytes=64) for half in range(2)]
         for h in range(2):
-            picked = gather_pair(h, HALF)
+            picked = keep.tile([P, 2, S], BF16, name="picked0_%d" % h)
+            for u in range(2):
+                scalar_gather(picked[:, u, :HALF], planes[2 * h + u], 0, HALF)
+                vector_gather(picked[:, u, HALF:], planes[2 * h + u], HALF, HALF)
             for half in range(2):
-                place(woven0[half], h, picked[:, :, HALF * half : HALF * (half + 1)])
+                weave(woven0[half], h, picked[:, :, HALF * half : HALF * (half + 1)])
         for half in range(2):
             quantise(0, HALF * half, HALF, woven0[half])
 
         woven1 = [keep.tile([P, 4 * QUARTER], BF16, name="woven1_%d" % q, align_bytes=64) for q in range(4)]
-        picked = gather_pair(2, 3 * QUARTER)
-        for q in range(4):
-            place(woven1[q], 0, picked[:, :, QUARTER * q : QUARTER * (q + 1)])
-        last = {q: keep.tile([P, 2, QUARTER], BF16, name="last%d" % q) for q in range(1, 4)}
-        for t in range(2):
-            gather(False, woven1[0][:].rearrange("p (n t) -> p n t", t=4)[:, :, 2 + t], planes[6 + t], 0, QUARTER)
+        low = [keep.tile([P, 2, QUARTER], BF16, name="picked1_0_%d" % q) for q in range(4)]
+        for u in range(2):
+            vector_gather(low[0][:, u, :], planes[4 + u], 0, QUARTER)
             for q in range(1, 4):
-                gather(True, last[q][:, t, :], planes[6 + t], QUARTER * q, QUARTER)
-        for half in range(2):
-            for q in (2 * half, 2 * half + 1):
-                if q in last:
-                    place(woven1[q], 1, last[q][:])
-            for q in (2 * half, 2 * half + 1):
+                scalar_gather(low[q][:, u, :], planes[4 + u], QUARTER * q, QUARTER)
+        for q in range(4):
+            weave(woven1[q], 0, low[q][:])
+
+        high = {q: keep.tile([P, 2, QUARTER], BF16, name="picked1_1_%d" % q) for q in range(1, 4)}
+        for u in range(2):
+            vector_gather(places(woven1[0])[:, :, 2 + u], planes[6 + u], 0, QUARTER)
+            for q in range(1, 4):
+                scalar_gather(high[q][:, u, :], planes[6 + u], QUARTER * q, QUARTER)
+        for quarters in ((0, 1), (2, 3)):
+            for q in quarters:
+                if q in high:
+                    weave(woven1[q], 1, high[q][:])
+            for q in quarters:
                 quantise(1, QUARTER * q, QUARTER, woven1[q])
 
         def new_bank(number):
@@ -149,17 +156,22 @@ def tile_picked_highway_tanh_l_kernel(
                 stop=stop,
             )
 
+        parts = [(0, 0), (0, 1), (1, 0), (1, 1)]
+        later_parts = parts[1:]
+        u_first = [new_bank(q) for q in range(2)]
+        u_y = {part: new_bank(2 + i) for i, part in enumerate(later_parts)}
+        u_gate = {part: new_bank(5 + i) for i, part in enumerate(later_parts)}
 
-        def new_tile(name, half):
-            return keep.tile([P, HALF], F32, name="%s%d" % (name, half))
+        def y_pass(part, z):
+            b, half = part
+            mx_pass(u_y[part][:], 0, b, HALF * half, z, z == 0, z == 1)
 
-
-        def turned_gate_pass(bank, part, z):
+        def turned_gate_pass(part, z):
             b, half = part
             for i in range(HALF // P):
                 j0 = HALF * half + P * i
                 nc.tensor.matmul_mx(
-                    out=bank[:, P * i : P * (i + 1)],
+                    out=u_gate[part][:, P * i : P * (i + 1)],
                     lhsT=x_codes[z][:, j0 : j0 + P].bitcast(FP8X4),
                     lhsT_scale=x_scale[z][:, j0 : j0 + P],
                     rhs=w_codes[1, z][:, P * b : P * (b + 1)].bitcast(FP8X4),
@@ -168,108 +180,101 @@ def tile_picked_highway_tanh_l_kernel(
                     stop=(z == 1 and i == HALF // P - 1),
                 )
 
-        def turn(bank, src, start, stop):
-            squares = src.shape[1] // P
-            for i in range(squares):
-                cols = slice(P * i, P * (i + 1))
-                nc.tensor.matmul(
-                    bank[:, cols], src[:, cols], ident[:], start=start and i == 0, stop=stop and i == squares - 1, is_transpose=True
-                )
-
-        parts = [(0, 0), (0, 1), (1, 0), (1, 1)]
-        first = [new_bank(0), new_bank(1)]
-        u_y = {part: new_bank(1 + i) for i, part in enumerate(parts) if i > 0}
-        u_g = {part: new_bank(4 + i) for i, part in enumerate(parts) if i > 0}
-
-        def y_pass(part, z):
-            mx_pass(u_y[part][:], 0, part[0], HALF * part[1], z, z == 0, z == 1)
-
         for q in range(2):
-            mx_pass(first[q][:, :QUARTER], 0, 0, QUARTER * q, 0, True, False)
-        for part in parts[1:]:
+            mx_pass(u_first[q][:, :QUARTER], 0, 0, QUARTER * q, 0, True, False)
+        for part in later_parts:
             y_pass(part, 0)
         for q in range(2):
-            mx_pass(first[q][:, QUARTER:], 1, 0, QUARTER * q, 0, False, False)
-        turned_gate_pass(u_g[1, 0], (1, 0), 0)
+            mx_pass(u_first[q][:, QUARTER:], 1, 0, QUARTER * q, 0, False, False)
+        turned_gate_pass((1, 0), 0)
         for q in range(2):
-            mx_pass(first[q][:, :QUARTER], 0, 0, QUARTER * q, 1, False, False)
-            mx_pass(first[q][:, QUARTER:], 1, 0, QUARTER * q, 1, False, True)
-        turned_gate_pass(u_g[1, 0], (1, 0), 1)
+            mx_pass(u_first[q][:, :QUARTER], 0, 0, QUARTER * q, 1, False, False)
+            mx_pass(u_first[q][:, QUARTER:], 1, 0, QUARTER * q, 1, False, True)
+        turned_gate_pass((1, 0), 1)
         for b in range(2):
-            turned_gate_pass(u_g[b, 1], (b, 1), 0)
+            turned_gate_pass((b, 1), 0)
         y_pass((0, 1), 1)
         for b in range(2):
-            turned_gate_pass(u_g[b, 1], (b, 1), 1)
+            turned_gate_pass((b, 1), 1)
         for half in range(2):
             y_pass((1, half), 1)
 
-        y = {part: new_tile("y%d_" % part[0], part[1]) for part in parts}
-        gate = {part: new_tile("gate%d_" % part[0], part[1]) for part in parts}
+        y = {part: keep.tile([P, HALF], F32, name="y%d_%d" % part) for part in parts}
+        sigmoid_out = {part: keep.tile([P, HALF], F32, name="sigmoid%d_%d" % part) for part in parts}
 
         def activate(dst, src, func):
             nc.scalar.activation(dst, src, func, bias=zero[:])
 
         for q in range(2):
             cols = slice(QUARTER * q, QUARTER * (q + 1))
-            activate(y[0, 0][:, cols], first[q][:, :QUARTER], TANH)
-            activate(gate[0, 0][:, cols], first[q][:, QUARTER:], SIGMOID)
-        activate(gate[1, 0][:], u_g[1, 0][:], SIGMOID)
+            activate(y[0, 0][:, cols], u_first[q][:, :QUARTER], TANH)
+            activate(sigmoid_out[0, 0][:, cols], u_first[q][:, QUARTER:], SIGMOID)
+        activate(sigmoid_out[1, 0][:], u_gate[1, 0][:], SIGMOID)
         activate(y[0, 1][:], u_y[0, 1][:], TANH)
-        activate(gate[0, 1][:], u_g[0, 1][:], SIGMOID)
-        activate(gate[1, 1][:], u_g[1, 1][:], SIGMOID)
+        for b in range(2):
+            activate(sigmoid_out[b, 1][:], u_gate[b, 1][:], SIGMOID)
         for half in range(2):
             activate(y[1, half][:], u_y[1, half][:], TANH)
-        turned = {part: gate[part] for part in parts[1:]}
-        for number, part in enumerate(parts[1:]):
+
+        gate = {parts[0]: sigmoid_out[parts[0]]}
+        for number, part in enumerate(later_parts):
             gate[part] = new_bank(number)
-            turn(gate[part], turned[part][:], True, True)
+            for i in range(HALF // P):
+                cols = slice(P * i, P * (i + 1))
+                nc.tensor.matmul(
+                    gate[part][:, cols],
+                    sigmoid_out[part][:, cols],
+                    ident[:],
+                    start=(i == 0),
+                    stop=(i == HALF // P - 1),
+                    is_transpose=True,
+                )
 
         def piece_of(tiles, piece):
             b, j0, n = piece
             half, c0 = divmod(j0, HALF)
             return tiles[b, half][:, c0 : c0 + n]
 
-        fused = [(0, 0, HALF), (0, HALF, HALF)]
-        split = [(1, 0, HALF), (1, HALF, QUARTER), (1, HALF + QUARTER, QUARTER)]
-        picked_r = {}
-        for b, j0, n in fused + split:
-            picked_r[b, j0, n] = keep.tile([P, n], F32, name="picked_r%d_%d" % (b, j0))
-        for b, j0, n in split:
-            nc.scalar.activation(picked_r[b, j0, n][:], res_rows[b][:].indirect(entries(j0, n)), COPY)
+        block0 = [(0, 0, HALF), (0, HALF, HALF)]
+        block1 = [(1, 0, HALF), (1, HALF, QUARTER), (1, HALF + QUARTER, QUARTER)]
 
-        def difference(piece):
+        looked_up = {}
+        for b, j0, n in block0 + block1:
+            looked_up[b, j0, n] = keep.tile([P, n], F32, name="looked_up%d_%d" % (b, j0))
+        for b, j0, n in block1:
+            scalar_gather(looked_up[b, j0, n][:], res_rows[b], j0, n)
+
+        e = dict(looked_up)
+        e[block1[0]] = sigmoid_out[1, 0]
+
+        def gather_and_subtract(piece):
             b, j0, n = piece
-            nc.vector.tensor_tensor(picked_r[piece][:], res_rows[b][:].indirect(entries(j0, n)), piece_of(y, piece), ALU.subtract)
+            nc.vector.tensor_tensor(looked_up[piece][:], res_rows[b][:].indirect(entries(j0, n)), piece_of(y, piece), ALU.subtract)
 
-        gated = {piece: picked_r[piece] for piece in fused + split}
-        gated[split[0]] = turned[1, 0]
-
-        def gated_r(piece):
-            nc.vector.scalar_tensor_tensor(gated[piece][:], piece_of(gate, piece), 1.0, picked_r[piece][:], ALU.subtract, ALU.mult)
-
-        def gated_y(piece):
-            nc.vector.tensor_tensor(piece_of(y, piece), piece_of(gate, piece), piece_of(y, piece), ALU.mult)
+        def make_e(piece):
+            nc.vector.scalar_tensor_tensor(e[piece][:], piece_of(gate, piece), 1.0, looked_up[piece][:], ALU.subtract, ALU.mult)
 
         def finish(engine, piece, c0, n, dst):
             b, j0 = piece[:2]
-            engine.tensor_tensor(dst, piece_of(y, (b, j0 + c0, n)), gated[piece][:, c0 : c0 + n], ALU.subtract)
+            engine.tensor_tensor(dst, piece_of(y, (b, j0 + c0, n)), e[piece][:, c0 : c0 + n], ALU.subtract)
             nc.sync.dma_start(out=out[P * b : P * (b + 1), j0 + c0 : j0 + c0 + n], in_=dst)
 
-        def finish_in_place(engine, piece, c0, n):
-            finish(engine, piece, c0, n, gated[piece][:, c0 : c0 + n])
+        def finish_over_e(engine, piece, c0, n):
+            finish(engine, piece, c0, n, e[piece][:, c0 : c0 + n])
 
-        for stage in (difference, gated_r):
-            for piece in fused:
-                stage(piece)
-        finish_in_place(nc.gpsimd, fused[0], 0, HALF)
-        finish_in_place(nc.gpsimd, fused[1], 0, HALF - EIGHTH)
+        for step in (gather_and_subtract, make_e):
+            for piece in block0:
+                step(piece)
+        finish_over_e(nc.gpsimd, block0[0], 0, HALF)
+        finish_over_e(nc.gpsimd, block0[1], 0, HALF - LEFT_TO_VECTOR)
         for half in range(2):
-            gated_y((1, HALF * half, HALF))
-        gated_r(split[0])
-        gated_r(split[1])
-        finish_in_place(nc.vector, split[0], 0, QUARTER)
-        gated_r(split[2])
-        finish(nc.vector, fused[1], HALF - EIGHTH, EIGHTH, picked_r[split[0]][:, :EIGHTH])
-        finish_in_place(nc.vector, split[0], QUARTER, QUARTER)
-        finish_in_place(nc.vector, split[1], 0, QUARTER)
-        finish_in_place(nc.vector, split[2], 0, QUARTER)
+            nc.vector.tensor_tensor(y[1, half][:], gate[1, half][:], y[1, half][:], ALU.mult)
+
+        make_e(block1[0])
+        make_e(block1[1])
+        finish_over_e(nc.vector, block1[0], 0, QUARTER)
+        make_e(block1[2])
+        finish(nc.vector, block0[1], HALF - LEFT_TO_VECTOR, LEFT_TO_VECTOR, looked_up[block1[0]][:, :LEFT_TO_VECTOR])
+        finish_over_e(nc.vector, block1[0], QUARTER, QUARTER)
+        for piece in block1[1:]:
+            finish_over_e(nc.vector, piece, 0, QUARTER)

@@ -78,9 +78,9 @@ def tile_picked_highway_tanh_l_kernel(
         nc.sync.dma_start(out=w1_codes[0][:], in_=w1_rows[:, 0, :])
         load_plane(7)
         nc.sync.dma_start(out=w2_codes[:], in_=w2_words.rearrange("z p n t -> p z (n t)").bitcast(I32))
-        nc.sync.dma_start(out=w1_codes[1][:], in_=w1_rows[:, 1, :])
         res_rows = []
         for b in range(2):
+            nc.sync.dma_start(out=w1_codes[1][:, P * b : P * (b + 1)], in_=w1_rows[:, 1, P * b : P * (b + 1)])
             rows = keep.tile([P, T], F32, name="res%d" % b)
             nc.sync.dma_start(out=rows[:], in_=res[P * b : P * (b + 1), :])
             res_rows.append(rows)

from contextlib import ExitStack

import concourse.mybir as mybir
from concourse.masks import make_identity

K, T, S, N = 1024, 2048, 1024, 256
FLOPS = 2 * 2 * K * N * S

F32 = mybir.dt.float32
BF16 = mybir.dt.bfloat16
I32 = mybir.dt.int32
U32 = mybir.dt.uint32
U16 = mybir.dt.uint16
U8 = mybir.dt.uint8
FP8X4 = mybir.dt.float8_e4m3fn_x4
ALU = mybir.AluOpType
TANH = mybir.ActivationFunctionType.Tanh
SIGMOID = mybir.ActivationFunctionType.Sigmoid
COPY = mybir.ActivationFunctionType.Copy

P = 128
HALF = 512
QUARTER = 256

LEFT_TO_VECTOR = 128


def tile_picked_highway_tanh_l_kernel(
    tc, xT, res, w1_words, w1_scales, w2_words, w2_scales, offs, out
):
    nc = tc.nc
    with ExitStack() as ctx:
        keep = ctx.enter_context(tc.tile_pool(name="keep", bufs=1))
        psum = ctx.enter_context(tc.psum_pool(name="psum", bufs=1))

        offsets = keep.tile([P, S // 16], U16, name="offsets")

        def entries(j0, n):
            return offsets[:, j0 // 16 : (j0 + n) // 16]

        staged = []
        for w, scales in enumerate((w1_scales, w2_scales)):
            rows = keep.tile([4, 2, 4, N // 4], I32, name="staged%d" % w)
            nc.scalar.dma_start(
                out=rows[:].rearrange("r z q n -> r (z q) n"),
                in_=scales.bitcast(I32).rearrange("z (q r) n -> r (z q) n", r=4),
            )
            staged.append(rows)

        far_left = keep.tile([P, 1], F32, name="far_left")
        zero = keep.tile([P, 1], F32, name="zero")
        nc.vector.memset(far_left[:], -200.0)
        nc.scalar.activation(zero[:], far_left[:], SIGMOID)

        ident = keep.tile([P, P], F32, name="ident")
        make_identity(nc, ident[:])

        w_scale = []
        for w in range(2):
            w_scale.append(keep.tile([P, 2, N], U8, name="w_scale%d" % w, align_bytes=64))
            nc.gpsimd.memset(w_scale[w][:].bitcast(I32), 0)

        x_rows = xT.rearrange("(z p t) c -> z t p c", p=P, t=4)
        w1_rows = w1_words.rearrange("z p n t -> p z (n t)").bitcast(I32)
        w1_codes = [keep.tile([P, N], I32, name="w1_codes%d" % z, align_bytes=64) for z in range(2)]
        w2_codes = keep.tile([P, 2, N], I32, name="w2_codes", align_bytes=64)
        w_codes = {(0, 0): w1_codes[0][:], (0, 1): w1_codes[1][:], (1, 0): w2_codes[:, 0, :], (1, 1): w2_codes[:, 1, :]}
        planes = []

        def load_plane(i):
            planes.append(keep.tile([P, T], F32, name="plane%d" % i))
            nc.sync.dma_start(out=planes[i][:], in_=x_rows[i // 4, i % 4])

        load_plane(0)
        nc.sync.dma_start(offsets[:], offs)
        for i in range(1, 7):
            load_plane(i)
        nc.sync.dma_start(out=w1_codes[0][:], in_=w1_rows[:, 0, :])
        load_plane(7)
        nc.sync.dma_start(out=w2_codes[:], in_=w2_words.rearrange("z p n t -> p z (n t)").bitcast(I32))
        res_rows = []
        for b in range(2):
            nc.sync.dma_start(out=w1_codes[1][:, P * b : P * (b + 1)], in_=w1_rows[:, 1, P * b : P * (b + 1)])
            rows = keep.tile([P, T], F32, name="res%d" % b)
            nc.sync.dma_start(out=rows[:], in_=res[P * b : P * (b + 1), :])
            res_rows.append(rows)

        for w in range(2):
            for q in range(4):
                nc.vector.tensor_copy(w_scale[w][32 * q : 32 * q + 4].bitcast(I32), staged[w][:, :, q, :])

        def scalar_gather(dst, window, j0, n):
            nc.scalar.activation(dst, window[:].indirect(entries(j0, n)), COPY)

        def vector_gather(dst, window, j0, n):
            nc.vector.tensor_copy(dst, window[:].indirect(entries(j0, n)))

        x_codes = [keep.tile([P, S], U32, name="x_codes%d" % z, align_bytes=64) for z in range(2)]
        x_scale = [keep.tile([P, S], U8, name="x_scale%d" % z, align_bytes=64) for z in range(2)]

        def places(woven):
            return woven[:].rearrange("p (n t) -> p n t", t=4)

        def weave(woven, h, two_planes):
            nc.vector.tensor_copy(places(woven)[:, :, 2 * h : 2 * h + 2], two_planes.rearrange("p u n -> p n u"))

        def quantise(z, j0, n, woven):
            nc.vector.quantize_mx(
                out=x_codes[z][:, j0 : j0 + n].bitcast(FP8X4), scales=x_scale[z][:, j0 : j0 + n], in_=woven[:]
            )

        woven0 = [keep.tile([P, 4 * HALF], BF16, name="woven0_%d" % half, align_bytes=64) for half in range(2)]
        for h in range(2):
            picked = keep.tile([P, 2, S], BF16, name="picked0_%d" % h)
            for u in range(2):
                scalar_gather(picked[:, u, :HALF], planes[2 * h + u], 0, HALF)
                vector_gather(picked[:, u, HALF:], planes[2 * h + u], HALF, HALF)
            for half in range(2):
                weave(woven0[half], h, picked[:, :, HALF * half : HALF * (half + 1)])
        for half in range(2):
            quantise(0, HALF * half, HALF, woven0[half])

        woven1 = [keep.tile([P, 4 * QUARTER], BF16, name="woven1_%d" % q, align_bytes=64) for q in range(4)]
        low = [keep.tile([P, 2, QUARTER], BF16, name="picked1_0_%d" % q) for q in range(4)]
        for u in range(2):
            vector_gather(low[0][:, u, :], planes[4 + u], 0, QUARTER)
            for q in range(1, 4):
                scalar_gather(low[q][:, u, :], planes[4 + u], QUARTER * q, QUARTER)
        for q in range(4):
            weave(woven1[q], 0, low[q][:])

        high = {q: keep.tile([P, 2, QUARTER], BF16, name="picked1_1_%d" % q) for q in range(1, 4)}
        for u in range(2):
            vector_gather(places(woven1[0])[:, :, 2 + u], planes[6 + u], 0, QUARTER)
            for q in range(1, 4):
                scalar_gather(high[q][:, u, :], planes[6 + u], QUARTER * q, QUARTER)
        for quarters in ((0, 1), (2, 3)):
            for q in quarters:
                if q in high:
                    weave(woven1[q], 1, high[q][:])
            for q in quarters:
                quantise(1, QUARTER * q, QUARTER, woven1[q])

        def new_bank(number):
            return psum.tile([P, HALF], F32, name="bank%d" % number)

        def mx_pass(dst, w, b, j0, z, start, stop):
            n = dst.shape[1]
            nc.tensor.matmul_mx(
                out=dst,
                lhsT=w_codes[w, z][:, P * b : P * (b + 1)].bitcast(FP8X4),
                lhsT_scale=w_scale[w][:, z, P * b : P * (b + 1)],
                rhs=x_codes[z][:, j0 : j0 + n].bitcast(FP8X4),
                rhs_scale=x_scale[z][:, j0 : j0 + n],
                start=start,
                stop=stop,
            )

        parts = [(0, 0), (0, 1), (1, 0), (1, 1)]
        later_parts = parts[1:]
        u_first = [new_bank(q) for q in range(2)]
        u_y = {part: new_bank(2 + i) for i, part in enumerate(later_parts)}
        u_gate = {part: new_bank(5 + i) for i, part in enumerate(later_parts)}

        def y_pass(part, z):
            b, half = part
            mx_pass(u_y[part][:], 0, b, HALF * half, z, z == 0, z == 1)

        def turned_gate_pass(part, z):
            b, half = part
            for i in range(HALF // P):
                j0 = HALF * half + P * i
                nc.tensor.matmul_mx(
                    out=u_gate[part][:, P * i : P * (i + 1)],
                    lhsT=x_codes[z][:, j0 : j0 + P].bitcast(FP8X4),
                    lhsT_scale=x_scale[z][:, j0 : j0 + P],
                    rhs=w_codes[1, z][:, P * b : P * (b + 1)].bitcast(FP8X4),
                    rhs_scale=w_scale[1][:, z, P * b : P * (b + 1)],
                    start=(z == 0 and i == 0),
                    stop=(z == 1 and i == HALF // P - 1),
                )

        for q in range(2):
            mx_pass(u_first[q][:, :QUARTER], 0, 0, QUARTER * q, 0, True, False)
        for part in later_parts:
            y_pass(part, 0)
        for q in range(2):
            mx_pass(u_first[q][:, QUARTER:], 1, 0, QUARTER * q, 0, False, False)
        turned_gate_pass((1, 0), 0)
        for q in range(2):
            mx_pass(u_first[q][:, :QUARTER], 0, 0, QUARTER * q, 1, False, False)
            mx_pass(u_first[q][:, QUARTER:], 1, 0, QUARTER * q, 1, False, True)
        turned_gate_pass((1, 0), 1)
        for b in range(2):
            turned_gate_pass((b, 1), 0)
        y_pass((0, 1), 1)
        for b in range(2):
            turned_gate_pass((b, 1), 1)
        for half in range(2):
            y_pass((1, half), 1)

        y = {part: keep.tile([P, HALF], F32, name="y%d_%d" % part) for part in parts}
        sigmoid_out = {part: keep.tile([P, HALF], F32, name="sigmoid%d_%d" % part) for part in parts}

        def activate(dst, src, func):
            nc.scalar.activation(dst, src, func, bias=zero[:])

        for q in range(2):
            cols = slice(QUARTER * q, QUARTER * (q + 1))
            activate(y[0, 0][:, cols], u_first[q][:, :QUARTER], TANH)
            activate(sigmoid_out[0, 0][:, cols], u_first[q][:, QUARTER:], SIGMOID)
        activate(sigmoid_out[1, 0][:], u_gate[1, 0][:], SIGMOID)
        activate(y[0, 1][:], u_y[0, 1][:], TANH)
        for b in range(2):
            activate(sigmoid_out[b, 1][:], u_gate[b, 1][:], SIGMOID)
        for half in range(2):
            activate(y[1, half][:], u_y[1, half][:], TANH)

        gate = {parts[0]: sigmoid_out[parts[0]]}
        for number, part in enumerate(later_parts):
            gate[part] = new_bank(number)
            for i in range(HALF // P):
                cols = slice(P * i, P * (i + 1))
                nc.tensor.matmul(
                    gate[part][:, cols],
                    sigmoid_out[part][:, cols],
                    ident[:],
                    start=(i == 0),
                    stop=(i == HALF // P - 1),
                    is_transpose=True,
                )

        def piece_of(tiles, piece):
            b, j0, n = piece
            half, c0 = divmod(j0, HALF)
            return tiles[b, half][:, c0 : c0 + n]

        block0 = [(0, 0, HALF), (0, HALF, HALF)]
        block1 = [(1, 0, HALF), (1, HALF, QUARTER), (1, HALF + QUARTER, QUARTER)]

        looked_up = {}
        for b, j0, n in block0 + block1:
            looked_up[b, j0, n] = keep.tile([P, n], F32, name="looked_up%d_%d" % (b, j0))
        for b, j0, n in block1:
            scalar_gather(looked_up[b, j0, n][:], res_rows[b], j0, n)

        e = dict(looked_up)
        e[block1[0]] = sigmoid_out[1, 0]

        def gather_and_subtract(piece):
            b, j0, n = piece
            nc.vector.tensor_tensor(looked_up[piece][:], res_rows[b][:].indirect(entries(j0, n)), piece_of(y, piece), ALU.subtract)

        def make_e(piece):
            nc.vector.scalar_tensor_tensor(e[piece][:], piece_of(gate, piece), 1.0, looked_up[piece][:], ALU.subtract, ALU.mult)

        def finish(engine, piece, c0, n, dst):
            b, j0 = piece[:2]
            engine.tensor_tensor(dst, piece_of(y, (b, j0 + c0, n)), e[piece][:, c0 : c0 + n], ALU.subtract)
            nc.sync.dma_start(out=out[P * b : P * (b + 1), j0 + c0 : j0 + c0 + n], in_=dst)

        def finish_over_e(engine, piece, c0, n):
            finish(engine, piece, c0, n, e[piece][:, c0 : c0 + n])

        for step in (gather_and_subtract, make_e):
            for piece in block0:
                step(piece)
        finish_over_e(nc.gpsimd, block0[0], 0, HALF)
        finish_over_e(nc.gpsimd, block0[1], 0, HALF - LEFT_TO_VECTOR)
        for half in range(2):
            nc.vector.tensor_tensor(y[1, half][:], gate[1, half][:], y[1, half][:], ALU.mult)

        make_e(block1[0])
        make_e(block1[1])
        finish_over_e(nc.vector, block1[0], 0, QUARTER)
        make_e(block1[2])
        finish(nc.vector, block0[1], HALF - LEFT_TO_VECTOR, LEFT_TO_VECTOR, looked_up[block1[0]][:, :LEFT_TO_VECTOR])
        finish_over_e(nc.vector, block1[0], QUARTER, QUARTER)
        for piece in block1[1:]:
            finish_over_e(nc.vector, piece, 0, QUARTER)
